import numpy as np, ml_dtypes
CORES = [2,3,42,43,82,83,122,123]
N = 8
import mx_ref
BF = ml_dtypes.bfloat16
def gentries(a):
    return np.ascontiguousarray(a.reshape(8, 16, -1).transpose(0, 2, 1)).reshape(8, -1)
def gtable(e):
    e = np.asarray(e); return np.ascontiguousarray(e.reshape(8, -1, 16).transpose(0, 2, 1)).reshape(128, -1).astype(np.int32)
def gcols(t, e):
    v = np.concatenate([t.reshape(8, 16, -1, 4), np.zeros((8, 16, 1, 4), BF)], axis=2)
    return np.ascontiguousarray(np.stack([v[g][:, e[g]] for g in range(8)])).reshape(128, -1)
def gpick(z, e):
    return np.concatenate([z[16 * g:16 * g + 16][:, e[g]] for g in range(8)])
def tile(rs):
    return np.stack(rs, axis=2).reshape(128, -1).astype(BF)
def pick(q, e):
    c = np.concatenate([q[0].reshape(128, -1, 4), np.zeros((128, 1, 4), np.uint8)], axis=1); s = np.concatenate([q[1], np.ones((16, 1), np.uint8)], axis=1)
    return (np.ascontiguousarray(c[:, e].reshape(128, -1)), np.ascontiguousarray(s[:, e]))
def join(*qs):
    return (np.concatenate([q[0] for q in qs], axis=1), np.concatenate([q[1] for q in qs], axis=1))
def put(q, e, v):
    c, s = q[0].reshape(128, -1, 4).copy(), q[1].copy(); c[:, e] = v[0].reshape(128, -1, 4); s[:, e] = v[1]
    return (c.reshape(128, -1), s)
def pk(c, s):
    return (np.ascontiguousarray(c), mx_ref.live(s))
def emit(q):
    return q[0], q[1]
def packed(v, rng):
    q = [mx_ref.quantize(np.ascontiguousarray(v[r])) for r in range(N)]
    return np.stack([a for a, b in q]), np.stack([mx_ref.plane(b, rng) for a, b in q])
def values_of_codes():
    e, c = np.zeros((128, 128, 4), np.float32), np.zeros((128, 2, 4), np.uint8)
    e[np.arange(128), np.arange(128), 0] = 1
    c[:127, :, 0] = np.arange(256).reshape(2, 128).T[:127]
    return mx_ref.matmul(mx_ref.quantize(e.reshape(128, 512).astype(BF)), (c.reshape(128, 8), np.full((16, 2), 127, np.uint8))).T.reshape(-1).astype(np.float64)
CODE_VALUE, SCALE_VALUE = values_of_codes(), 2.0 ** (np.arange(256) - 127.0)
def decode(q):
    return (CODE_VALUE[q[0]].reshape(16, 8, -1, 4) * SCALE_VALUE[q[1]][:, None, :, None] + 0.0).reshape(128, -1).astype(np.float32)
def f(rng, *shape):
    return mx_ref.flush((rng.standard_normal(shape, dtype=np.float32) * np.exp2(rng.integers(-2, 3, shape[:-1] + (1,)))).astype(BF))
def wide(rng, *shape, cols=0):
    v = rng.standard_normal(shape, dtype=np.float32) * np.exp2(rng.integers(-12, 13, shape)).astype(np.float32)
    if cols: v *= np.repeat(np.exp2(rng.integers(-cols, cols + 1, shape[:-2] + (1, shape[-1] // 4))) * (rng.random(shape[:-2] + (1, shape[-1] // 4)) > 0.0625), 4, axis=-1).astype(np.float32)
    return mx_ref.flush(v.astype(BF))
C = 320
STEP = [1, 2, 4]
def numbers_of(rng):
    return {"x": np.array(f(rng, N, 128, 4 * C)), "u": np.array(f(rng, N, 128, 512)), "v": np.array(f(rng, N, 128, 512))}
def orders(rng):
    return rng.permuted(np.tile(np.arange(C), (N, 8, 1)), axis=2)
def mates(rng):
    e = orders(rng)
    m = np.zeros_like(e)
    np.put_along_axis(m, e[:, :, 0::2], e[:, :, 1::2], axis=2)
    np.put_along_axis(m, e[:, :, 1::2], e[:, :, 0::2], axis=2)
    return m
def stored(c, a, m):
    return {"cl": np.stack([gtable(c[r]) for r in range(N)]), "pl": np.stack([gtable(a[r]) for r in range(N)]), "ml": np.stack([gtable(m[r]) for r in range(N)])}
def lists(rng):
    return stored(orders(rng), orders(rng), mates(rng))
def layers(rng, still=[]):
    w = np.array(f(rng, N, 128, 2048)).reshape(N, 8, 16, 4, 8, 16, 4)
    for i in still:
        w[:, :, i] = 0
        w[:, :, :, :, :, i] = 0
    return w
def weights(rng, w):
    c, s = packed(np.ascontiguousarray(w).reshape(N, 128, 2048), rng)
    return {"wc": c, "ws": s}
def setup_inputs(rng):
    return {**numbers_of(rng), **lists(rng), **weights(rng, layers(rng))}
def setup_inputs_ties(rng):
    d = numbers_of(rng)
    o = rng.permutation(N)
    k = rng.integers(0, 4, (N, 8, C))
    k[o[1]] -= 4
    k[o[2], rng.permutation(8)[:4]] = 1
    x = d["x"].reshape(N, 8, 16, C, 4)
    x[:, :, 0] = 0
    x[:, :, 0, :, 0] = k.astype(np.float32).astype(BF)
    u = d["u"].reshape(N, 128, 128, 4)
    u[:, :, ::16] = 0
    for r in range(N):
        for h in range(0, 128, 16): u[r, h, h, 0] = 0.0 if r == o[0] else 1.0
    c, a, m = orders(rng), orders(rng), mates(rng)
    c[o[3]] = m[o[3]]
    return {"x": x.reshape(N, 128, 4 * C), "u": u.reshape(N, 128, 512), "v": d["v"], **stored(c, a, m), **weights(rng, layers(rng, [0]))}
def setup_inputs_near(rng):
    d = numbers_of(rng)
    x = d["x"].astype(np.float32).reshape(N, 8, 16, C, 4)
    x[:, :, 0] = 0
    x[:, :, 8:] = 0
    u = d["u"].reshape(N, 128, 128, 4)
    u[:, :, ::16] = 0
    o = (np.arange(N) + rng.integers(4)) % 4
    for r in range(N):
        c = rng.choice([-1.0, 1.0], (8, 1))
        s = rng.integers(0, 16, (8, C))
        digits = ((s[:, :, None] >> np.arange(4)) & 1) * np.exp2(np.arange(4) - 23.0)
        if o[r] < 2:
            x[r, :, 0, :, 0] = c
            x[r, :, 8] = digits
            x[r, :, 11, :, 0] = 2.0 ** -10
        elif o[r] == 2: x[r, :, 8] = digits * rng.choice([-1.0, 1.0], (8, C, 1))
        else:
            x[r, :, 8, :, 0] = np.where(s < 8, 1.25, 0.0) * 2.0 ** -29 * c
            x[r, :, 9, :, 0] = np.where(s < 8, 0.0, 1.125) * 2.0 ** -29 * c
            for g in rng.permutation(8)[:4]:
                e = rng.choice([-1.0, 1.0], C) * 2.0 ** -29
                x[r, g, 8, :, 0] = 1.25 * e
                x[r, g, 9, :, 0] = -1.125 * e
        if o[r] >= 2: x[r, :, 12, :, 0] = np.where(rng.random((8, C)) < 0.5, 1.0, 1.5) * 2.0 ** -30
        at = [0, C - 1, int(rng.integers(C)), int(rng.integers(C))]
        for g, j in zip(rng.permutation(8)[:4], at): x[r, g, 0, j, 0] = 2.0 ** 29 * rng.choice([-1.0, 1.0])
        k = 1.0 if o[r] == 0 else 2.0 ** -30
        for h in range(0, 128, 16):
            u[r, h, h, 0] = k if o[r] < 2 else 1.0
            if o[r] < 2: u[r, h + 11, h, 0] = k
            if o[r] < 3: u[r, h + 8, h] = k
            else:
                u[r, h + 8, h, 0] = k
                u[r, h + 9, h, 0] = 1.125 * k
                u[r, h + 10, h, 0] = k
    w = layers(rng, [0, 8, 9, 10, 11, 12, 13, 14, 15])
    for g in range(8): w[:, g, 12, 0, g, 10, 0] = 2.0 ** -8
    return {"x": x.reshape(N, 128, 4 * C).astype(BF), "u": u.reshape(N, 128, 512), "v": d["v"], **lists(rng), **weights(rng, w)}
def setup_inputs_odd(rng):
    d = numbers_of(rng)
    k = (N, 8, 2, 8, C, 4)
    x = (1.0 + (2 * rng.integers(0, 64, k) + 1) * 2.0 ** -7) * np.exp2(-rng.integers(0, 7, k).astype(np.float64)) * rng.choice([-1.0, 1.0], k)
    x[:, :, 0, 0, :, 0] = 1.96875 * 2.0 ** 8 * rng.choice([-1.0, 1.0], (N, 8, C))
    x[:, :, 1, 0, :, 0] = np.where(rng.random((N, 8, C)) < 0.5, 1.875, 0.09375) * 2.0 ** 8
    u = d["u"].reshape(N, 8, 2, 8, 128, 4)
    u[:, :, :, 0, ::16] = 0
    for r in range(N):
        for i, g in enumerate(rng.permutation(8)[:4]):
            x[r, g, 0, 1, :, 0] = (8 + rng.integers(0, 2, C)) * 2.0 ** (i - 8)
            u[r, :, :, :, 16 * g] = 0
            u[r, g, 0, 1, 16 * g, 0] = 1.0
    return {"x": x.astype(np.float32).reshape(N, 128, 4 * C).astype(BF), "u": u.reshape(N, 128, 512), "v": d["v"], **lists(rng), **weights(rng, layers(rng, [0, 8]))}
def setup_inputs_ends(rng):
    d = numbers_of(rng)
    x = np.zeros((N, 8, 16, C, 4))
    u = d["u"].astype(np.float32).reshape(N, 128, 128, 4)
    v = d["v"].astype(np.float32)
    w = np.zeros((N, 128, 4, 128, 4), np.float32)
    o, e = rng.permutation(N) % 4, rng.permutation(N) % 4
    i = np.arange(128)
    for r in range(N):
        h = rng.permutation(8)
        s = np.where(h < 2, 0.0, h % 2 * 2.0 - 1.0)[None, :, None]
        high = (0.9 + 0.1 * rng.random((8, 16, C, 4))) * 2.0 ** 30
        if o[r] == 0: x[r] = -high
        if o[r] == 1: x[r] = high * rng.choice([-1.0, 1.0], (1, 1, C, 1))
        if o[r] == 2: x[r] = -(1.0 + 0.125 * rng.integers(0, 8, (8, 16, C, 4))) * 2.0 ** -30
        if o[r] == 3: x[r] = d["x"][r].astype(np.float32).reshape(8, 16, C, 4)[:, :, :1]
        if o[r] < 2:
            x[r, :, 15] = 0
            u[r, :, ::16] = s * (0.9 + 0.1 * rng.random((128, 8, 4))) * 2.0 ** 30
            v[r] = rng.choice([-1.0, 1.0], (128, 512)) * (0.9 + 0.1 * rng.random((128, 512))) * 2.0 ** 30
        if o[r] == 2:
            u[r, :, ::16] = s * (1.0 + 0.125 * rng.integers(0, 8, (128, 8, 4))) * 2.0 ** -30
            v[r] = rng.choice([-1.0, 1.0], (128, 512)) * (1.0 + 0.125 * rng.integers(0, 8, (128, 512))) * 2.0 ** -30
        if o[r] == 3: u[r, :, ::16] *= np.abs(s).astype(np.float32)
        k = np.full(128, [-0.125, -0.125, 0.25, 2.0 ** -8][o[r]])
        if o[r] >= 2: k[15::16] = 2.0 ** 8
        for b in range(4): w[r, i, b, i, b] = k
    c, a, m = orders(rng), orders(rng), mates(rng)
    j = np.arange(C)
    c[e == 0], m[e == 0] = j, j ^ 1
    c[e == 1], m[e == 1] = C - 1 - j, C - 1 - j
    c[e == 2], a[e == 2], m[e == 2] = C - 1 - j, j, (j + C // 2) % C
    return {"x": x.astype(np.float32).reshape(N, 128, 4 * C).astype(BF), "u": u.reshape(N, 128, 512).astype(BF), "v": v.astype(BF), **stored(c, a, m), **weights(rng, w.astype(BF))}
def setup_inputs_spread(rng):
    d = setup_inputs(rng)
    d["x"] = wide(rng, N, 128, 4 * C, cols=6)
    return d
def check_inputs(d):
    b = []
    for k in ("x", "u", "v"):
        a = np.abs(d[k].astype(np.float32))
        if not (np.isfinite(a).all() and ((a == 0) | (a >= 2.0 ** -30) & (a <= 2.0 ** 30)).all()): b.append("a value of " + k)
    j = np.arange(C)
    for k in ("cl", "pl", "ml"):
        for r in range(N):
            e = gentries(d[k][r])
            if not (np.sort(e, axis=1) == j).all(): b.append("a list of " + k)
            elif k == "ml" and ((at(e, e) != j) | (e == j)).any(): b.append("ml: mates")
    none, least, most = [emit(mx_ref.quantize(np.full((128, 16), k, np.float32).astype(BF)))[1][0, 0] for k in (0.0, 2.0 ** -8, 2.0 ** 8)]
    for r in range(N):
        if ((d["wc"][r] == 0x7F) | (d["wc"][r] == 0xFF)).any(): b.append("wc: a code that is no number")
        s = mx_ref.live(d["ws"][r])
        if ((s != none) & ((s < least) | (s > most))).any(): b.append("ws: a scale out of range")
        if (((d["wc"][r].reshape(16, 8, 512, 4) & 0x7F) != 0) & (s == none)[:, None, :, None]).any(): b.append("wc: a code other than zero under the scale of zeros")
    return b
def at(a, e):
    return np.take_along_axis(a, e, axis=1)
def above(s, a, b):
    return (at(s, a) > at(s, b)) | (at(s, a) == at(s, b)) & (a < b)
def reference(x, u, v, cl, pl, ml, wc, ws):
    qu = [mx_ref.quantize(u[r]) for r in range(N)]
    lay = [pk(wc[r], ws[r]) for r in range(N)]
    child, parent, mate = [gentries(cl[r]) for r in range(N)], [gentries(pl[r]) for r in range(N)], [gentries(ml[r]) for r in range(N)]
    j = np.tile(np.arange(C), (8, 1))
    now = [x[r] for r in range(N)]
    for step in STEP:
        t, z = [], []
        for r in range(N):
            q = mx_ref.quantize(now[r])
            s = mx_ref.matmul(qu[r], q)[::16] + np.float32(0.0)
            c, m = child[r], mate[r]
            o = np.where(above(s, j, m) == above(s, c, at(c, m)), c, at(c, m))
            new = np.argsort(o, axis=1)
            k = at(o, at(np.argsort(parent[r], axis=1), at(m, at(parent[r], new))))
            t.append(decode(q))
            p = t[r].astype(BF)
            z.append(mx_ref.quantize(((gcols(p, new).astype(np.float32) + gcols(p, k).astype(np.float32)) * np.float32(0.5)).astype(BF)))
            parent[r], mate[r] = new, k
        for r in range(N):
            h = [mx_ref.matmul(pick(lay[r], np.arange(128 * b, 128 * b + 128)), z[(r - step) % N]) * np.float32(0.03125) for b in range(4)]
            now[r] = tile([t[r][:, b::4] + gpick(h[b], parent[r]) for b in range(4)])
    y, co = np.zeros((N, 128, C), np.float32), np.zeros((N, 8, C), np.float32)
    oc, osc = np.zeros((N, 128, 4 * C), np.uint8), np.zeros((N, 16, C), np.uint8)
    for r in range(N):
        q = mx_ref.quantize(now[r])
        y[r] = mx_ref.matmul(mx_ref.quantize(v[r]), q)
        co[r] = mate[r]
        oc[r], osc[r] = emit(q)
    return {"y": y, "co": co, "oc": oc, "osc": osc}

@@ -1,0 +1,391 @@
+from concourse.bass import DstId, RemoteDMATransfer
+from concourse.mybir import dt, AluOpType as Op, ActivationFunctionType as Fn
+
+C = 320
+H = C // 2
+STEP = [1, 2, 4]
+ROUNDS = 3
+HZ = 192
+S0 = 2.0 ** -70
+X4, F32, B16, I32, U16, U8 = "float8_e4m3fn_x4", "float32", "bfloat16", "int32", "uint16", "uint8"
+
+SCRATCH = {}
+for _names, _w, _d in (
+        ("idf id512 ids", C, F32), ("idb mask keep t16 w1k", C, B16), ("wts", 2 * C, B16), ("pcol qi", 1, I32), ("qf", 1, F32),
+        ("c16", 20, F32), ("pk", 8, I32), ("pku", 8, U16), ("fours dia less dib", 16, B16), ("thr inv", 16, F32), ("ein", 516, B16),
+        ("eq", 512, X4), ("es", 512, U8),
+        ("xin", 4 * C, B16), ("uin vin", 512, B16), ("ci32 mi32 pi32", 20, I32), ("cu mu pu", 20, U16),
+        ("wq", 512, X4), ("wsc", 512, U8), ("uq uq2 vq", 128, X4), ("us us2 vs", 128, U8),
+        ("crep thb an am pp tpr", C, B16), ("cir w0 pir", C, F32), ("wx", 14 * C, F32), ("ciu ap thu m2u", 20, U16), ("jc jc0", 40, F32),
+        ("sc ga gb f0 f1 kco yt rg", C, F32), ("bits zz", 2 * C, B16), ("lst", 80, U16), ("sm", 340, F32), ("mg", 60, I32),
+        ("bg", 2 * C, F32), ("ph", 4 * C, B16), ("tb", 4 * C, B16),
+        ("tp vp rp", 4 * C, F32), ("tq tk zt xt", 4 * C, B16), ("zq", C, X4), ("zs", C, U8)):
+    for _n in _names.split():
+        SCRATCH[_n] = ("sbuf", [128, _w], _d)
+for _r in range(ROUNDS + 1):
+    SCRATCH["xq%d" % _r] = ("sbuf", [128, C], X4)
+    SCRATCH["xs%d" % _r] = ("sbuf", [128, C], U8)
+for _r in range(ROUNDS):
+    SCRATCH["lq%d" % _r] = ("sbuf", [128, C], X4)
+    SCRATCH["ls%d" % _r] = ("sbuf", [128, C], U8)
+    for _n in ("lk", "lv", "lz", "kp", "vl", "zl"):
+        SCRATCH["%s%d" % (_n, _r)] = ("sbuf", [128, 20], U16)
+SCRATCH["psa"] = ("psum", [128, 2048], F32)
+SCRATCH["psb"] = ("psum", [128, 2048], F32)
+
+LOADS = ["x", "u", "v", "cl", "pl", "ml", "wc", "ws"]
+SEMAPHORES = ["V", "A", "P", "G", "sent", "ost"] + ["d" + k for k in LOADS] + ["%s%d" % (k, r) for k in ("arq", "ark", "arv", "arz") for r in range(ROUNDS)]
+
+
+def rank_program(g, core, T, topo):
+    rank = T.rank_of(core)
+    if rank is None:
+        return
+    queues = {"V": g.vector, "A": g.scalar, "P": g.tensor, "G": g, "S": g.sync}
+    count = {k: 0 for k in queues}
+    seen = {k: {} for k in queues}
+    known = {}
+
+    def need(q, deps):
+        for sem, val in sorted(set(deps), key=lambda t: -t[1]):
+            if seen[q].get(sem, 0) >= val:
+                continue
+            queues[q].wait_ge(T.sem[sem], val)
+            seen[q][sem] = val
+            for s2, v2 in known.get((sem, val), {}).items():
+                if seen[q].get(s2, 0) < v2:
+                    seen[q][s2] = v2
+
+    def run(q, deps, call, *args, **kw):
+        need(q, deps)
+        call(*args, **kw).then_inc(T.sem[q], 1)
+        count[q] += 1
+        known[(q, count[q])] = dict(seen[q])
+        return (q, count[q])
+
+    def vfill(ap, k): return run("V", (), g.vector.memset, ap, k)
+    def vcp(out, in_, *deps): return run("V", deps, g.vector.tensor_copy, out, in_)
+    def vtt(out, a, b, op, *deps): return run("V", deps, g.vector.tensor_tensor, out, a, b, op)
+    def vts(out, a, s, op, *deps): return run("V", deps, g.vector.tensor_scalar, out, a, s, None, op)
+    def vts2(out, a, s, op, s2, op2, *deps): return run("V", deps, g.vector.tensor_scalar, out, a, s, s2, op, op2)
+    def vscan(out, w, x, *deps): return run("V", deps, g.vector.tensor_tensor_scan, out, w, x, 0.0, Op.mult, Op.add)
+    def vqt(out, sc, x, *deps): return run("V", deps, g.vector.quantize_mx, out, sc, x)
+    def acp(out, in_, *deps): return run("A", deps, g.scalar.activation, out, in_, Fn.Copy)
+    def asc(out, in_, k, *deps): return run("A", deps, g.scalar.activation, out, in_, Fn.Copy, scale=k)
+    def mm(out, w, ws, x, xs, *deps): return run("P", deps, g.tensor.matmul_mx, out, w, ws, x, xs, True, True)
+
+    def load(queue, name, out, in_):
+        queue.dma_start(out, in_).then_inc(T.sem["d" + name], 16)
+        return ("d" + name, 16)
+
+    def R(name, r): return T["%s%d" % (name, r)]
+    def pl(b): return slice(C * b, C * b + C)
+    def bank(ps, b): return ps[:, 512 * b:512 * b + C]
+    def w128(b): return slice(128 * b, 128 * b + 128)
+    def gat(t, lst): return t[:, 0:C].indirect(lst[:, 0:20])
+
+    sent = [0]
+
+    def send(r, out, src, sem, *deps):
+        need("G", deps)
+        dst = T.cores[(rank + STEP[r]) % len(T.cores)]
+        rid, pid, _ = topo.addr(dst)
+        eng = topo.engines(core, dst)[:8]
+        g.remote_dma(out, src, T.sem[sem], T.sem.sent, pid, rid, sum(1 << e for e in eng))
+        sent[0] += len(eng)
+
+    later = []
+
+    def fill(n=99):
+        for _ in range(min(n, len(later))):
+            later.pop(0)()
+
+    dc = load(g.scalar, "cl", T.ci32[:], T.cl[:])
+    dp = load(g.scalar, "pl", T.pi32[:], T.pl[:])
+    dm = load(g.scalar, "ml", T.mi32[:], T.ml[:])
+    dx = load(g.sync, "x", T.xin[:], T.x[:])
+    du = load(g.sync, "u", T.uin[:], T.u[:])
+    dwc = load(g.sync, "wc", T.wq[:].bitcast(dt.uint8), T.wc[:])
+    dws = load(g.sync, "ws", T.wsc[:], T.ws[:])
+    dv = load(g.sync, "v", T.vin[:], T.v[:])
+
+    def iota(buf, pattern, base, cm, flag=True):
+        kw = {"allow_small_or_imprecise_dtypes": True} if flag else {}
+        return run("G", (), g.iota, buf[:], pattern, base, cm, **kw)
+    i_p = iota(T.pcol, [[0, 1]], 0, 1, False)
+    i_c = iota(T.c16, [[16, 20]], 0, 0)
+    i_t = iota(T.t16, [[0, 20], [1, 16]], 0, 0)
+    i_b = iota(T.idb, [[1, C]], -160, 0)
+    i_k = iota(T.pk, [[16, 8]], 0, 0, False)
+    t_e1 = vfill(T.ein[:], 1.0)
+    t_fo = vfill(T.fours[:], 4.0)
+    i_e = run("G", [t_e1], g.affine_select, T.ein[:], T.ein[:], [[1, 516]], Op.is_equal, 0.0, -3, -4)
+    i_f = iota(T.idf, [[1, C]], 0, 0)
+    i_5 = iota(T.id512, [[512, C]], 0, 0)
+
+    tqi = vts(T.qi[:], T.pcol[:], 15, Op.bitwise_and, i_p)
+    tqf = vcp(T.qf[:], T.qi[:], tqi)
+    tj = vts(T.jc[:, 0:20], T.c16[:], T.qf[:, 0:1], Op.add, i_c, tqf)
+    tj0 = vts(T.jc0[:, 20:40], T.c16[:], T.qf[:, 0:1], Op.add, i_c, tqf)
+    tmask = vts(T.mask[:], T.t16[:], T.qf[:, 0:1], Op.is_equal, i_t, tqf)
+    tkeep = vts(T.keep[:], T.t16[:], 0.0, Op.not_equal, i_t)
+    twt = [vts2(T.wts[:, h:h + C], T.t16[:], T.qf[:, 0:1], Op.not_equal, 4.0, Op.mult, i_t, tqf) for h in (0, C)]
+    tdi = vts2(T.dia[:], T.t16[:, 0:16], T.qf[:, 0:1], Op.is_equal, 0.6, Op.mult, i_t, tqf)
+    tth = vscan(T.thr[:], T.fours[:], T.dia[:], t_fo, tdi)
+    tw1 = vts2(T.w1k[:], T.t16[:], T.qf[:, 0:1], Op.is_gt, 1024.0, Op.mult, i_t, tqf)
+    tdj = vts2(T.dib[:], T.t16[:, 0:16], T.qf[:, 0:1], Op.is_equal, 1.0 / S0, Op.mult, i_t, tqf)
+    t_le = vfill(T.less[:], 2.0 ** -10)
+    tinv = vscan(T.inv[:], T.less[:], T.dib[:], t_le, tdj)
+    tcu = vcp(T.cu[:], T.ci32[:], dc)
+    tj1 = vcp(T.jc0[:, 0:20], T.ci32[:], dc)
+    tcrep = acp(T.crep[:], gat(T.idb, T.cu), i_b, tcu)
+    tpu = vcp(T.pu[:], T.pi32[:], dp)
+    tan = vcp(T.an[:, 0:C].indirect(T.pu[:, 0:20]), T.idb[:], i_b, tpu)
+    tmu = vcp(T.mu[:], T.mi32[:], dm)
+    tg0 = vcp(T.mg[:, 20:40], T.mi32[:], dm)
+
+    def wrap16(src, off, out, col, *deps):
+        s = {}
+        def a(): s[1] = vtt(T.tb[:, col:col + C], src.indirect(off), T.mask[:], Op.mult, tmask, *deps)
+        def b(): s[2] = vscan(T.tb[:, col + C:col + 2 * C], T.keep[:], T.tb[:, col:col + C], s[1], tkeep)
+        def c(): s[3] = vts(out, T.tb[:, col + C + 15:col + 2 * C:16], 160.0, Op.add, s[2])
+        return s, a, b, c
+
+    def pickx(i, src, off, *deps):
+        return run("A", deps, g.scalar.activation, T.wx[:, 2 * C * i:2 * C * i + C], src.indirect(off), Fn.Identity, bias=160 * S0, scale=S0)
+
+    def scanx(i, src, *deps):
+        return vscan(T.wx[:, 2 * C * i + C:2 * C * i + 2 * C], T.w1k[:], src if src is not None else T.wx[:, 2 * C * i:2 * C * i + C], tw1, *deps)
+
+    def readx(i, out, tok):
+        return vts2(out, T.wx[:, 2 * C * i + C + 15:2 * C * i + 2 * C:16], T.inv[:, 15:16], Op.mult, 0.05, Op.add, tok, tinv)
+
+    st = {}
+
+    def rest(jc, tjc, tmg):
+        mg, sm = T.mg, T.sm
+        def s5(): st[5] = vtt(sm[:, 0:40], jc[:], mg[:, 0:40], Op.min, *tmg(), *tjc())
+        def s6(): st[6] = vtt(sm[:, 40:80], jc[:], mg[:, 0:40], Op.max, *tmg(), *tjc())
+        def s7(): st["l"] = vcp(T.lst[:], sm[:, 0:80], st[5], st[6])
+        def s8(): st["d"] = vtt(sm[:, 80:120], jc[:], mg[:, 0:40], Op.subtract, *tmg(), *tjc())
+        def s9(): st[9] = vts(sm[:, 120:160], sm[:, 80:120], 0.0, Op.is_lt, st["d"])
+        def s10(): st["q"] = vtt(sm[:, 160:180], sm[:, 120:140], sm[:, 140:160], Op.is_equal, st[9])
+        return [s5, s6, s8, s7, s9, s10]
+
+    te, tci = [], {}
+
+    def unpacker(b):
+        te.append(vqt(T.eq[:, w128(b)], T.es[:, w128(b)], T.ein[:, 3 - b:515 - b], i_e))
+
+    def inverse():
+        s = {}
+        def o(): s[0] = vcp(T.cir[:, 0:C].indirect(T.cu[:, 0:20]), T.ids[:], tids, tcu)
+        def b(): s[2] = scanx(2, T.cir[:], s[0])
+        def c(): tci["u"] = readx(2, T.ciu[:], s[2])
+        return [o, b, c]
+
+    tx_cm = pickx(0, T.crep[:, 0:C], T.mu[:, 0:20], tcrep, tmu)
+    tam = acp(T.am[:], gat(T.an, T.mu), tan, tmu)
+    tx_kp = pickx(1, T.am[:, 0:C], T.pu[:, 0:20], tam)
+    tx = [vqt(T.xq0[:, h:h + H], T.xs0[:, h:h + H], T.xin[:, 4 * h:4 * (h + H)], dx) for h in (0, H)]
+    t_cm = scanx(0, None, tx_cm)
+    tpk = vcp(T.pku[:], T.pk[:], i_k)
+    tuq = vqt(T.uq[:], T.us[:], T.uin[:], du)
+    t_cm = readx(0, T.mg[:, 0:20], t_cm)
+    later.extend(rest(T.jc0, lambda: (tj0, tj1), lambda: (t_cm, tg0)))
+    fill(2)
+    tu1 = vcp(T.uq2[:, 0:128].bitcast(dt.uint32), T.uq[:, 0:128].bitcast(dt.uint32).indirect(T.pku[:, 0:8]), tuq, tpk)
+    tu2 = acp(T.us2[:, 0:128], T.us[:, 0:128].indirect(T.pku[:, 0:8]), tuq, tpk)
+    tids = asc(T.ids[:], T.idf[:], S0, i_f)
+    fill()
+    send(0, R("lq", 0)[:, 0:C].bitcast(dt.uint8), T.xq0[:, 0:C].bitcast(dt.uint8), "arq0", *tx)
+    send(0, R("ls", 0)[:, 0:C], T.xs0[:, 0:C], "arq0", *tx)
+
+    t_tq, t_rp, tX, tkp, tkk = [], [()] * 4, [], None, None
+    for r in range(ROUNDS):
+        last = r + 1 == ROUNDS
+        xq, xs, lst, sm, mg, vl, zl = R("xq", r), R("xs", r), T.lst, T.sm, T.mg, R("vl", r), R("zl", r)
+        lk, lv, lz = R("lk", r), R("lv", r), R("lz", r)
+        arq, ark, arv, arz = ("arq%d" % r, 16), ("ark%d" % r, 8), ("arv%d" % r, 8), ("arz%d" % r, 8)
+
+        def own(b): return mm(bank(T.psa, b), T.eq[:, w128(b)], T.es[:, w128(b)], xq[:, 0:C], xs[:, 0:C], te[b], *tx, *t_rp[b])
+
+        ps = [mm(T.psb[:, 512 * h:512 * h + H], T.uq2[:], T.us2[:], xq[:, H * h:H * h + H], xs[:, H * h:H * h + H], tx[h], tu1, tu2, *t_tq) for h in (0, 1)]
+        if r:
+            pt = [own(b) for b in range(4)]
+        fill()
+        ts = [vcp(T.sc[:, 0:H], T.psb[:, 0:H], ps[0]), acp(T.sc[:, H:C], T.psb[:, 512:512 + H], ps[1])]
+        if r:
+            tkp = scanx(4 + r, None, tx_kp)
+        tl = st["l"]
+        tga = acp(T.ga[:], T.sc[:, 0:C].indirect(lst[:, 20:40]), *ts, tl)
+        tgb1 = acp(T.gb[:, H:C], T.sc[:, 0:C].indirect(lst[:, 10:20]), *ts, tl)
+        tgb0 = vcp(T.gb[:, 0:H], T.sc[:, 0:C].indirect(lst[:, 0:10]), *ts, tl)
+        ttp, kps = {}, {}
+        if r:
+            tkp = readx(4 + r, R("kp", r)[:], tkp)
+            send(r, R("lk", r)[:], R("kp", r)[:], "ark%d" % r, tkp)
+            tpir = acp(T.pir[:], gat(T.crep, R("kp", r)), tkp)
+            for b in range(3):
+                ttp[b] = acp(T.tp[:, pl(b)], bank(T.psa, b), pt[b], *tX)
+        else:
+            tpp = acp(T.pp[:], gat(T.am, T.pu), tam)
+            def q1(): kps[2] = scanx(1, None, tx_kp)
+            def q2(): kps[3] = readx(1, R("kp", 0)[:], kps[2])
+            later.extend([q1, lambda: unpacker(0), q2] + [lambda b=b: unpacker(b) for b in range(1, 4)])
+            fill(1)
+        tb0 = vtt(T.bits[:, 0:H], T.sc[:, 0:C].indirect(lst[:, 40:50]), T.gb[:, 0:H], Op.is_le, tgb0)
+        tb2 = vtt(T.bits[:, C:2 * C], T.sc[:, 0:C].indirect(lst[:, 60:80]), T.ga[:], Op.is_le, tga)
+        tb1 = vtt(T.bits[:, H:C], T.sc[:, 0:C].indirect(lst[:, 50:60]), T.gb[:, H:C], Op.is_le, tgb1)
+        fill(1)
+        tz = vscan(T.zz[:], T.wts[:], T.bits[:], *twt, tb0, tb1, tb2)
+        fill(1)
+        e1 = vts(sm[:, 180:220], T.zz[:, 15:2 * C:16], T.thr[:, 15:16], Op.is_ge, tz, tth)
+        fill(1)
+        e2 = vtt(sm[:, 220:240], sm[:, 180:200], sm[:, 200:220], Op.is_equal, e1)
+        fill(1)
+        e3 = vtt(sm[:, 240:260], sm[:, 220:240], sm[:, 160:180], Op.is_equal, e2, st["q"])
+        fill(1)
+        e4 = vtt(sm[:, 260:280], sm[:, 240:260], sm[:, 80:100], Op.mult, e3, st["d"])
+        f4 = vtt(sm[:, 300:320], sm[:, 240:260], sm[:, 100:120], Op.mult, e3, st["d"])
+        fill(1)
+        e5 = vtt(sm[:, 280:300], sm[:, 260:280], mg[:, 0:20], Op.add, e4)
+        f5 = vtt(sm[:, 320:340], sm[:, 300:320], mg[:, 20:40], Op.add, f4)
+        tvl = vcp(vl[:], sm[:, 280:300], e5)
+        tap = vcp(T.ap[:] if r else T.thu[:], sm[:, 320:340], f5)
+        if r == 0:
+            send(0, R("lk", 0)[:], R("kp", 0)[:], "ark0", kps[3])
+        send(r, R("lv", r)[:], vl[:], "arv%d" % r, tvl)
+
+        def neighbour(): return [mm(bank(T.psb, b), T.eq[:, w128(b)], T.es[:, w128(b)], R("lq", r)[:], R("ls", r)[:], arq, *ts) for b in range(4)]
+        tq, tk, tv = {}, {}, {}
+
+        def pick(b): tk[b] = acp(T.tk[:, pl(b)], T.tq[:, pl(b)].indirect(lk[:, 0:20]), tq[b], ark)
+        def aevac(b): tq[b] = asc(T.tq[:, pl(b)], bank(T.psb, b), 0.5, pq[b])
+        def vevac(b): tq[b] = vts(T.tq[:, pl(b)], bank(T.psb, b), 0.5, Op.mult, pq[b])
+        def addv(b): tv[b] = vtt(T.vp[:, pl(b)], T.tq[:, pl(b)].indirect(lv[:, 0:20]), T.tk[:, pl(b)], Op.add, tq[b], tk[b], arv)
+        def zcols(b, c0, c1): return T.zt[:, 4 * c0 + b:4 * c1:4], T.vp[:, pl(b)].indirect(lz[:, c0 // 16:c1 // 16])
+
+        table = T.idf if last else T.w0
+
+        def next_lists():
+            def m(): st["m"] = vtt(T.bg[:, 0:C], gat(T.f1, T.ciu), T.mask[:], Op.mult, tf1, tci["u"])
+            def n0(): st[0] = vscan(T.bg[:, C:2 * C], T.keep[:], T.bg[:, 0:C], st["m"])
+            def n1(): st[1] = vcp(T.mg[:, 40:60], T.bg[:, C + 15:2 * C:16], st[0])
+            def n2(): st[2] = vts(T.mg[:, 0:20], T.mg[:, 40:60], 9, Op.logical_shift_right, st[1])
+            def n3(): st[3] = vts(T.mg[:, 20:40], T.mg[:, 40:60], 511, Op.bitwise_and, st[1])
+            def n4(): st[4] = vcp(T.m2u[:], T.mg[:, 0:20], st[2])
+            return [m, n0, n1, n2] + ([n4] if r else []) + [n3] + rest(T.jc, lambda: (tj, tci["f"]), lambda: (st[2], st[3]))
+
+        if r == 0:
+            later.extend(inverse())
+            pt = [own(b) for b in range(4)]
+            for b in range(3):
+                ttp[b] = acp(T.tp[:, pl(b)], bank(T.psa, b), pt[b])
+            tt0 = acp(T.tpr[:], gat(T.pp, T.thu), tpp, tap)
+            tthb = acp(T.thb[:], gat(T.idb, T.thu), tap)
+            pq = neighbour()
+            tph = acp(T.ph[:, 0:C], gat(T.idb, vl), tvl, i_b)
+            tkk = acp(T.ph[:, C:2 * C], T.ph[:, 0:C].indirect(vl[:, 0:20]), tph)
+            aevac(0)
+            aevac(1)
+            pick(0)
+            fill()
+            pick(1)
+            s, a, b, c = wrap16(T.tpr[:, 0:C], T.ciu[:, 0:20], zl[:], 0, tt0, tci["u"])
+            s2, a2, b2, c2 = wrap16(T.thb[:, 0:C], T.ciu[:, 0:20], T.ap[:], 2 * C, tthb, tci["u"])
+            a()
+            tci["f"] = vcp(T.jc[:, 20:40], T.ciu[:], tci["u"])
+            b()
+            c()
+            tzl = s[3]
+            send(0, R("lz", 0)[:], zl[:], "arz0", tzl)
+            a2()
+            tw0 = vtt(T.w0[:], gat(T.id512, T.cu), T.idf[:], Op.add, i_5, i_f, tcu)
+            b2()
+            vevac(2)
+            c2()
+            vevac(3)
+            tap = s2[3]
+            pick(2)
+            pick(3)
+            tf0 = acp(T.f0[:], gat(table, vl), tvl, tw0)
+        else:
+            pq = neighbour()
+            fill()
+            s, a, b, c = wrap16(T.pir[:, 0:C], vl[:, 0:20], zl[:], 0, tpir, tvl)
+            a()
+            b()
+            c()
+            tzl = s[3]
+            send(r, R("lz", r)[:], zl[:], "arz%d" % r, tzl)
+            tf0 = acp(T.f0[:], gat(table, vl), tvl, tw0, i_f)
+            if last:
+                tvq = vqt(T.vq[:], T.vs[:], T.vin[:], dv)
+            else:
+                tph = acp(T.ph[:, 0:C], gat(T.idb, vl), tvl, i_b)
+            aevac(0)
+            vevac(1)
+            pick(0)
+            vevac(2)
+            pick(1)
+            vevac(3)
+            pick(2)
+            pick(3)
+        for b in range(4):
+            addv(b)
+        t_tq = [tq[b] for b in range(4)]
+        za = [acp(*zcols(0, 0, C), tv[0], arz), acp(*zcols(1, 0, C), tv[1]), acp(*zcols(2, 0, HZ), tv[2])]
+        zv = [vcp(*zcols(2, HZ, C), tv[2], arz), vcp(*zcols(3, HZ, C), tv[3]), vcp(*zcols(3, 0, HZ), tv[3])]
+        tz1 = vqt(T.zq[:, HZ:C], T.zs[:, HZ:C], T.zt[:, 4 * HZ:4 * C], *zv, za[1])
+        tz0 = vqt(T.zq[:, 0:HZ], T.zs[:, 0:HZ], T.zt[:, 0:4 * HZ], *zv, *za)
+        if last:
+            tco = acp(T.kco[:], gat(T.f0, zl), tf0, tzl)
+            need("S", [tco])
+            g.sync.dma_start(T.co[:], T.kco[0:128:16, :]).then_inc(T.sem.ost, 16)
+        else:
+            tf1 = acp(T.f1[:], gat(T.f0, zl), tf0, tzl)
+            later.extend(next_lists())
+        order = [0, 1, 3, 2]
+        pr, tr = {}, {}
+        for b in order:
+            pr[b] = mm(bank(T.psb if b == 3 else T.psa, b), T.wq[:, w128(b)], T.wsc[:, w128(b)], T.zq[:], T.zs[:], dwc, dws, tz0, tz1, tq[3] if b == 3 else ttp[b])
+        fill(2)
+        for b in order:
+            tr[b] = asc(T.rp[:, pl(b)], bank(T.psb if b == 3 else T.psa, b), 0.03125, pr[b], *tX)
+        trg = acp(T.rg[:], T.rp[:, pl(3)].indirect(T.ap[:, 0:20]), tr[3], tap)
+        tX = []
+        for b in range(3):
+            tX.append(vtt(T.xt[:, b:4 * C:4], T.rp[:, pl(b)].indirect(T.ap[:, 0:20]), T.tp[:, pl(b)], Op.add, tr[b], ttp[b], tap))
+            fill(1)
+        tX.append(vtt(T.xt[:, 3:4 * C:4], T.rg[:], bank(T.psa, 3), Op.add, trg, pt[3]))
+        t_rp = [[tr[0]], [tr[1]], [tr[2]], [tX[3]]]
+        t_tq = t_tq + [tr[3]]
+        if not last:
+            if r == 0:
+                tkk = acp(T.ph[:, 2 * C:3 * C], T.ph[:, C:2 * C].indirect(zl[:, 0:20]), tkk, tzl)
+            else:
+                tkk = acp(T.ph[:, 2 * C:3 * C], T.ph[:, 0:C].indirect(T.m2u[:, 0:20]), tph, st[4])
+            tkk = acp(T.ph[:, 3 * C:4 * C], T.ph[:, 2 * C:3 * C].indirect((vl if r else T.ap)[:, 0:20]), tkk, tap)
+            tx_kp = pickx(5 + r, T.ph[:, 3 * C:4 * C], T.ciu[:, 0:20], tkk)
+        nq, ns = R("xq", r + 1), R("xs", r + 1)
+        tx = [vqt(nq[:, h:h + H], ns[:, h:h + H], T.xt[:, 4 * h:4 * (h + H)], *tX) for h in (0, H)]
+        if not last:
+            n = r + 1
+            send(n, R("lq", n)[:, 0:C].bitcast(dt.uint8), nq[:, 0:C].bitcast(dt.uint8), "arq%d" % n, *tx)
+            send(n, R("ls", n)[:, 0:C], ns[:, 0:C], "arq%d" % n, *tx)
+
+    need("S", tx)
+    g.sync.dma_start(T.oc[:, 0:4 * C], T.xq3[:, 0:C].bitcast(dt.uint8)).then_inc(T.sem.ost, 16)
+    for k in range(4):
+        g.sync.dma_start(T.osc[4 * k:4 * k + 4, 0:C], T.xs3[32 * k:32 * k + 4, 0:C]).then_inc(T.sem.ost, 16)
+    py = [mm(T.psb[:, 512 * h:512 * h + H], T.vq[:], T.vs[:], T.xq3[:, H * h:H * h + H], T.xs3[:, H * h:H * h + H], tx[h], tvq, *t_tq) for h in (0, 1)]
+    ty0 = vcp(T.yt[:, 0:H], T.psb[:, 0:H], py[0])
+    ty1 = acp(T.yt[:, H:C], T.psb[:, 512:512 + H], py[1])
+    need("S", [ty0])
+    g.sync.dma_start(T.y[:, 0:H], T.yt[:, 0:H]).then_inc(T.sem.ost, 16)
+    need("A", [ty1])
+    g.scalar.dma_start(T.y[:, H:C], T.yt[:, H:C]).then_inc(T.sem.ost, 16)
+    need("G", [(q, count[q]) for q in ("V", "A", "P", "G")])
+    g.wait_ge(T.sem.ost, 16 * 8)
+    g.wait_ge(T.sem.sent, sent[0])

@@ -1,4 +1,3 @@
-from concourse.bass import DstId, RemoteDMATransfer
 from concourse.mybir import dt, AluOpType as Op, ActivationFunctionType as Fn
 
 C = 320
@@ -6,19 +5,19 @@ H = C // 2
 STEP = [1, 2, 4]
 ROUNDS = 3
 HZ = 192
-S0 = 2.0 ** -70
+BIG = 2.0 ** 40
+TWO = 2048
 X4, F32, B16, I32, U16, U8 = "float8_e4m3fn_x4", "float32", "bfloat16", "int32", "uint16", "uint8"
 
 SCRATCH = {}
 for _names, _w, _d in (
-        ("idf id512 ids", C, F32), ("idb mask keep t16 w1k", C, B16), ("wts", 2 * C, B16), ("pcol qi", 1, I32), ("qf", 1, F32),
-        ("c16", 20, F32), ("pk", 8, I32), ("pku", 8, U16), ("fours dia less dib", 16, B16), ("thr inv", 16, F32), ("ein", 516, B16),
-        ("eq", 512, X4), ("es", 512, U8),
+        ("idf idk", C, F32), ("t16 wa wb w16", 16, B16), ("wts", 2 * C, B16), ("pcol qi", 1, I32), ("qf q1 inv invk", 1, F32), ("z40", 40, F32), ("qu", 40, U16),
+        ("pk", 8, I32), ("pku", 8, U16), ("ein", 516, B16), ("eq", 512, X4), ("es", 512, U8),
         ("xin", 4 * C, B16), ("uin vin", 512, B16), ("ci32 mi32 pi32", 20, I32), ("cu mu pu", 20, U16),
         ("wq", 512, X4), ("wsc", 512, U8), ("uq uq2 vq", 128, X4), ("us us2 vs", 128, U8),
-        ("crep thb an am pp tpr", C, B16), ("cir w0 pir", C, F32), ("wx", 14 * C, F32), ("ciu ap thu m2u", 20, U16), ("jc jc0", 40, F32),
-        ("sc ga gb f0 f1 kco yt rg", C, F32), ("bits zz", 2 * C, B16), ("lst", 80, U16), ("sm", 340, F32), ("mg", 60, I32),
-        ("bg", 2 * C, F32), ("ph", 4 * C, B16), ("tb", 4 * C, B16),
+        ("w0 g1 pw mw f0 f1 zp zm", C, F32), ("ar za f2 ze", C, B16), ("pwu eu", 20, U16), ("full", 40, I32), ("four", 80, I32), ("lh", 80, F32), ("dd", 20, F32),
+        ("lst", 80, U16), ("ch", 200, F32), ("cho", 100, F32),
+        ("sc ga gb kco yt rg", C, F32), ("bits zz", 2 * C, B16),
         ("tp vp rp", 4 * C, F32), ("tq tk zt xt", 4 * C, B16), ("zq", C, X4), ("zs", C, U8)):
     for _n in _names.split():
         SCRATCH[_n] = ("sbuf", [128, _w], _d)
@@ -28,13 +27,29 @@ for _r in range(ROUNDS + 1):
 for _r in range(ROUNDS):
     SCRATCH["lq%d" % _r] = ("sbuf", [128, C], X4)
     SCRATCH["ls%d" % _r] = ("sbuf", [128, C], U8)
-    for _n in ("lk", "lv", "lz", "kp", "vl", "zl"):
+    for _n in ("lv", "la", "vl", "ap"):
         SCRATCH["%s%d" % (_n, _r)] = ("sbuf", [128, 20], U16)
 SCRATCH["psa"] = ("psum", [128, 2048], F32)
 SCRATCH["psb"] = ("psum", [128, 2048], F32)
 
-LOADS = ["x", "u", "v", "cl", "pl", "ml", "wc", "ws"]
-SEMAPHORES = ["V", "A", "P", "G", "sent", "ost"] + ["d" + k for k in LOADS] + ["%s%d" % (k, r) for k in ("arq", "ark", "arv", "arz") for r in range(ROUNDS)]
+LOADS = ["x0", "x1", "u", "v", "cl", "pl", "ml", "wc", "ws"]
+SEMAPHORES = ["V", "A", "P", "G", "sent", "ost"] + ["d" + k for k in LOADS] + ["%s%d" % (k, r) for k in ("arq", "arv", "ara") for r in range(ROUNDS)]
+
+START = """pu ai mu g1 g2 qa cu qb sendq w0 pku ze e3 pwu e2 uq e1 f1 e0 uq2 pw zp mw zm us2 S0 S1 T bo0 bo1 an sh mn mx s0 dd lst s1
+           lo2 sum lo1b.V al hi1b hi2 lo1a hi1a t3 t2 dif bscan sig chain l1 sendl t0 t1"""
+MID = """f0 scat ascan g1 a1 senda f1 Tn f2 o0.V o2 o1.V tw0.V tw1.V ze v0 eu o3 pk2 v1 pk3 v2 v3
+         z2l.V z3l.V mw z0 z1 z2h.V z3h ql qh R0 R1 R2 R3 zm pw zp bo1 bo0 an r0 x0 r1 x1 r2 x2 r3 x3 sh qa S0 qb sendq S1 T
+         mn mx dd lst s1.V al s0 lo2 lo1a.V lo1b sum hi1a t0 t1 hi2 hi1b bscan dif t2 sig chain pwu l1 sendl t3"""
+LAST = """scat ascan a1 senda f0 Tn o0 o2 o3 pk2 o1.V tw0.V vq pk3 tw1.V v0 v1 z0 z1 v2 v3 z3h z2l.V z3l.V z2h.V kco co ql qh
+          R0 R1 R2 R3 r0.V x0 r1 x1 r2 x2 r3 x3 qb Y1 qa Y0 oc y1.V sy1 y0.V sy0 osc"""
+
+
+def cols(name, lo=0, hi=None, step=1):
+    return (name, lo, SCRATCH[name][1][1] if hi is None else hi, step)
+
+
+def by(win, lst):
+    return (win, lst)
 
 
 def rank_program(g, core, T, topo):
@@ -45,9 +60,11 @@ def rank_program(g, core, T, topo):
     count = {k: 0 for k in queues}
     seen = {k: {} for k in queues}
     known = {}
+    wrote = {n: [] for n in SCRATCH}
+    read = {n: [] for n in SCRATCH}
 
-    def need(q, deps):
-        for sem, val in sorted(set(deps), key=lambda t: -t[1]):
+    def need(q, marks):
+        for sem, val in sorted(set(marks), key=lambda t: -t[1]):
             if seen[q].get(sem, 0) >= val:
                 continue
             queues[q].wait_ge(T.sem[sem], val)
@@ -56,336 +73,216 @@ def rank_program(g, core, T, topo):
                 if seen[q].get(s2, 0) < v2:
                     seen[q][s2] = v2
 
-    def run(q, deps, call, *args, **kw):
-        need(q, deps)
-        call(*args, **kw).then_inc(T.sem[q], 1)
+    def meet(a, b):
+        if a[2] <= b[1] or b[2] <= a[1]:
+            return False
+        return a[3] != b[3] or (a[1] - b[1]) % a[3] == 0
+
+    def touch(outs, ins):
+        w, r = [], []
+        for o in outs:
+            w.append(o if len(o) == 4 else o[0])
+            r += [] if len(o) == 4 else [o[1]]
+        for i in ins:
+            r += [i] if len(i) == 4 else list(i)
+        bank = lambda v: (v[0], v[1] // 512 * 512, v[1] // 512 * 512 + 512, 1)
+        w = [bank(v) if v[0][:2] == "ps" else v for v in w] + [bank(v) for v in r if v[0][:2] == "ps"]
+        return w, [v for v in r if v[0][:2] != "ps"]
+
+    def before(w, r):
+        return [m for v in w + r for u, m in wrote[v[0]] if meet(u, v)] + [m for v in w for u, m in read[v[0]] if meet(u, v)]
+
+    def ap(v, cast=None):
+        if not isinstance(v, tuple):
+            return v
+        if len(v) == 2:
+            return ap(v[0], cast).indirect(ap(v[1]))
+        a = T[v[0]][:, v[1]:v[2]:v[3]] if v[3] > 1 else T[v[0]][:, v[1]:v[2]]
+        return a.bitcast(cast) if cast else a
+
+    def run(q, outs, ins, call):
+        w, r = touch(outs, [i for i in ins if isinstance(i, tuple)])
+        need(q, before(w, r))
+        call().then_inc(T.sem[q], 1)
         count[q] += 1
         known[(q, count[q])] = dict(seen[q])
-        return (q, count[q])
+        for v in w:
+            wrote[v[0]].append((v, (q, count[q])))
+        for v in r:
+            read[v[0]].append((v, (q, count[q])))
 
-    def vfill(ap, k): return run("V", (), g.vector.memset, ap, k)
-    def vcp(out, in_, *deps): return run("V", deps, g.vector.tensor_copy, out, in_)
-    def vtt(out, a, b, op, *deps): return run("V", deps, g.vector.tensor_tensor, out, a, b, op)
-    def vts(out, a, s, op, *deps): return run("V", deps, g.vector.tensor_scalar, out, a, s, None, op)
-    def vts2(out, a, s, op, s2, op2, *deps): return run("V", deps, g.vector.tensor_scalar, out, a, s, s2, op, op2)
-    def vscan(out, w, x, *deps): return run("V", deps, g.vector.tensor_tensor_scan, out, w, x, 0.0, Op.mult, Op.add)
-    def vqt(out, sc, x, *deps): return run("V", deps, g.vector.quantize_mx, out, sc, x)
-    def acp(out, in_, *deps): return run("A", deps, g.scalar.activation, out, in_, Fn.Copy)
-    def asc(out, in_, k, *deps): return run("A", deps, g.scalar.activation, out, in_, Fn.Copy, scale=k)
-    def mm(out, w, ws, x, xs, *deps): return run("P", deps, g.tensor.matmul_mx, out, w, ws, x, xs, True, True)
+    def vfill(o, k): run("V", [o], [], lambda: g.vector.memset(ap(o), k))
+    def vcp(o, i, cast=None): run("V", [o], [i], lambda: g.vector.tensor_copy(ap(o, cast), ap(i, cast)))
+    def vtt(o, a, b, op): run("V", [o], [a, b], lambda: g.vector.tensor_tensor(ap(o), ap(a), ap(b), op))
+    def vts(o, a, s, op): run("V", [o], [a, s], lambda: g.vector.tensor_scalar(ap(o), ap(a), ap(s), None, op))
+    def vts2(o, a, s, op, s2, op2): run("V", [o], [a, s, s2], lambda: g.vector.tensor_scalar(ap(o), ap(a), ap(s), ap(s2), op, op2))
+    def vscan(o, w, x): run("V", [o], [w, x], lambda: g.vector.tensor_tensor_scan(ap(o), ap(w), ap(x), 0.0, Op.mult, Op.add))
+    def vqt(o, s, x): run("V", [o, s], [x], lambda: g.vector.quantize_mx(ap(o), ap(s), ap(x)))
+    def mm(o, w, ws, x, xs): run("P", [o], [w, ws, x, xs], lambda: g.tensor.matmul_mx(ap(o), ap(w), ap(ws), ap(x), ap(xs), True, True))
 
-    def load(queue, name, out, in_):
-        queue.dma_start(out, in_).then_inc(T.sem["d" + name], 16)
-        return ("d" + name, 16)
+    def cp(q, o, i, k=None):
+        if q == "V":
+            vcp(o, i) if k is None else vts(o, i, k, Op.mult)
+        else:
+            run("A", [o], [i], lambda: g.scalar.activation(ap(o), ap(i), Fn.Copy, **({} if k is None else {"scale": k})))
 
-    def R(name, r): return T["%s%d" % (name, r)]
-    def pl(b): return slice(C * b, C * b + C)
-    def bank(ps, b): return ps[:, 512 * b:512 * b + C]
-    def w128(b): return slice(128 * b, 128 * b + 128)
-    def gat(t, lst): return t[:, 0:C].indirect(lst[:, 0:20])
+    def iota(o, pattern, base=0):
+        kw = {} if SCRATCH[o][2] == I32 else {"allow_small_or_imprecise_dtypes": True}
+        run("G", [cols(o)], [], lambda: g.iota(T[o][:], pattern[1:], base, pattern[0], **kw))
+
+    def load(q, name, o, src, cast=None):
+        queues[q].dma_start(ap(o, cast), src).then_inc(T.sem["d" + name], 16)
+        wrote[o[0]].append((o, ("d" + name, 16)))
+
+    stores = [0]
+
+    def store(q, out, v, src):
+        need(q, before([], [v]))
+        queues[q].dma_start(out, src).then_inc(T.sem.ost, 16)
+        stores[0] += 16
 
     sent = [0]
 
-    def send(r, out, src, sem, *deps):
-        need("G", deps)
+    def send(r, land, src, sem, cast=None):
+        need("G", before([], [src]))
         dst = T.cores[(rank + STEP[r]) % len(T.cores)]
         rid, pid, _ = topo.addr(dst)
         eng = topo.engines(core, dst)[:8]
-        g.remote_dma(out, src, T.sem[sem], T.sem.sent, pid, rid, sum(1 << e for e in eng))
+        g.remote_dma(ap(land, cast), ap(src, cast), T.sem[sem], T.sem.sent, pid, rid, sum(1 << e for e in eng))
         sent[0] += len(eng)
 
-    later = []
-
-    def fill(n=99):
-        for _ in range(min(n, len(later))):
-            later.pop(0)()
-
-    dc = load(g.scalar, "cl", T.ci32[:], T.cl[:])
-    dp = load(g.scalar, "pl", T.pi32[:], T.pl[:])
-    dm = load(g.scalar, "ml", T.mi32[:], T.ml[:])
-    dx = load(g.sync, "x", T.xin[:], T.x[:])
-    du = load(g.sync, "u", T.uin[:], T.u[:])
-    dwc = load(g.sync, "wc", T.wq[:].bitcast(dt.uint8), T.wc[:])
-    dws = load(g.sync, "ws", T.wsc[:], T.ws[:])
-    dv = load(g.sync, "v", T.vin[:], T.v[:])
-
-    def iota(buf, pattern, base, cm, flag=True):
-        kw = {"allow_small_or_imprecise_dtypes": True} if flag else {}
-        return run("G", (), g.iota, buf[:], pattern, base, cm, **kw)
-    i_p = iota(T.pcol, [[0, 1]], 0, 1, False)
-    i_c = iota(T.c16, [[16, 20]], 0, 0)
-    i_t = iota(T.t16, [[0, 20], [1, 16]], 0, 0)
-    i_b = iota(T.idb, [[1, C]], -160, 0)
-    i_k = iota(T.pk, [[16, 8]], 0, 0, False)
-    t_e1 = vfill(T.ein[:], 1.0)
-    t_fo = vfill(T.fours[:], 4.0)
-    i_e = run("G", [t_e1], g.affine_select, T.ein[:], T.ein[:], [[1, 516]], Op.is_equal, 0.0, -3, -4)
-    i_f = iota(T.idf, [[1, C]], 0, 0)
-    i_5 = iota(T.id512, [[512, C]], 0, 0)
-
-    tqi = vts(T.qi[:], T.pcol[:], 15, Op.bitwise_and, i_p)
-    tqf = vcp(T.qf[:], T.qi[:], tqi)
-    tj = vts(T.jc[:, 0:20], T.c16[:], T.qf[:, 0:1], Op.add, i_c, tqf)
-    tj0 = vts(T.jc0[:, 20:40], T.c16[:], T.qf[:, 0:1], Op.add, i_c, tqf)
-    tmask = vts(T.mask[:], T.t16[:], T.qf[:, 0:1], Op.is_equal, i_t, tqf)
-    tkeep = vts(T.keep[:], T.t16[:], 0.0, Op.not_equal, i_t)
-    twt = [vts2(T.wts[:, h:h + C], T.t16[:], T.qf[:, 0:1], Op.not_equal, 4.0, Op.mult, i_t, tqf) for h in (0, C)]
-    tdi = vts2(T.dia[:], T.t16[:, 0:16], T.qf[:, 0:1], Op.is_equal, 0.6, Op.mult, i_t, tqf)
-    tth = vscan(T.thr[:], T.fours[:], T.dia[:], t_fo, tdi)
-    tw1 = vts2(T.w1k[:], T.t16[:], T.qf[:, 0:1], Op.is_gt, 1024.0, Op.mult, i_t, tqf)
-    tdj = vts2(T.dib[:], T.t16[:, 0:16], T.qf[:, 0:1], Op.is_equal, 1.0 / S0, Op.mult, i_t, tqf)
-    t_le = vfill(T.less[:], 2.0 ** -10)
-    tinv = vscan(T.inv[:], T.less[:], T.dib[:], t_le, tdj)
-    tcu = vcp(T.cu[:], T.ci32[:], dc)
-    tj1 = vcp(T.jc0[:, 0:20], T.ci32[:], dc)
-    tcrep = acp(T.crep[:], gat(T.idb, T.cu), i_b, tcu)
-    tpu = vcp(T.pu[:], T.pi32[:], dp)
-    tan = vcp(T.an[:, 0:C].indirect(T.pu[:, 0:20]), T.idb[:], i_b, tpu)
-    tmu = vcp(T.mu[:], T.mi32[:], dm)
-    tg0 = vcp(T.mg[:, 20:40], T.mi32[:], dm)
-
-    def wrap16(src, off, out, col, *deps):
-        s = {}
-        def a(): s[1] = vtt(T.tb[:, col:col + C], src.indirect(off), T.mask[:], Op.mult, tmask, *deps)
-        def b(): s[2] = vscan(T.tb[:, col + C:col + 2 * C], T.keep[:], T.tb[:, col:col + C], s[1], tkeep)
-        def c(): s[3] = vts(out, T.tb[:, col + C + 15:col + 2 * C:16], 160.0, Op.add, s[2])
-        return s, a, b, c
-
-    def pickx(i, src, off, *deps):
-        return run("A", deps, g.scalar.activation, T.wx[:, 2 * C * i:2 * C * i + C], src.indirect(off), Fn.Identity, bias=160 * S0, scale=S0)
-
-    def scanx(i, src, *deps):
-        return vscan(T.wx[:, 2 * C * i + C:2 * C * i + 2 * C], T.w1k[:], src if src is not None else T.wx[:, 2 * C * i:2 * C * i + C], tw1, *deps)
-
-    def readx(i, out, tok):
-        return vts2(out, T.wx[:, 2 * C * i + C + 15:2 * C * i + 2 * C:16], T.inv[:, 15:16], Op.mult, 0.05, Op.add, tok, tinv)
-
-    st = {}
-
-    def rest(jc, tjc, tmg):
-        mg, sm = T.mg, T.sm
-        def s5(): st[5] = vtt(sm[:, 0:40], jc[:], mg[:, 0:40], Op.min, *tmg(), *tjc())
-        def s6(): st[6] = vtt(sm[:, 40:80], jc[:], mg[:, 0:40], Op.max, *tmg(), *tjc())
-        def s7(): st["l"] = vcp(T.lst[:], sm[:, 0:80], st[5], st[6])
-        def s8(): st["d"] = vtt(sm[:, 80:120], jc[:], mg[:, 0:40], Op.subtract, *tmg(), *tjc())
-        def s9(): st[9] = vts(sm[:, 120:160], sm[:, 80:120], 0.0, Op.is_lt, st["d"])
-        def s10(): st["q"] = vtt(sm[:, 160:180], sm[:, 120:140], sm[:, 140:160], Op.is_equal, st[9])
-        return [s5, s6, s8, s7, s9, s10]
-
-    te, tci = [], {}
-
-    def unpacker(b):
-        te.append(vqt(T.eq[:, w128(b)], T.es[:, w128(b)], T.ein[:, 3 - b:515 - b], i_e))
-
-    def inverse():
-        s = {}
-        def o(): s[0] = vcp(T.cir[:, 0:C].indirect(T.cu[:, 0:20]), T.ids[:], tids, tcu)
-        def b(): s[2] = scanx(2, T.cir[:], s[0])
-        def c(): tci["u"] = readx(2, T.ciu[:], s[2])
-        return [o, b, c]
-
-    tx_cm = pickx(0, T.crep[:, 0:C], T.mu[:, 0:20], tcrep, tmu)
-    tam = acp(T.am[:], gat(T.an, T.mu), tan, tmu)
-    tx_kp = pickx(1, T.am[:, 0:C], T.pu[:, 0:20], tam)
-    tx = [vqt(T.xq0[:, h:h + H], T.xs0[:, h:h + H], T.xin[:, 4 * h:4 * (h + H)], dx) for h in (0, H)]
-    t_cm = scanx(0, None, tx_cm)
-    tpk = vcp(T.pku[:], T.pk[:], i_k)
-    tuq = vqt(T.uq[:], T.us[:], T.uin[:], du)
-    t_cm = readx(0, T.mg[:, 0:20], t_cm)
-    later.extend(rest(T.jc0, lambda: (tj0, tj1), lambda: (t_cm, tg0)))
-    fill(2)
-    tu1 = vcp(T.uq2[:, 0:128].bitcast(dt.uint32), T.uq[:, 0:128].bitcast(dt.uint32).indirect(T.pku[:, 0:8]), tuq, tpk)
-    tu2 = acp(T.us2[:, 0:128], T.us[:, 0:128].indirect(T.pku[:, 0:8]), tuq, tpk)
-    tids = asc(T.ids[:], T.idf[:], S0, i_f)
-    fill()
-    send(0, R("lq", 0)[:, 0:C].bitcast(dt.uint8), T.xq0[:, 0:C].bitcast(dt.uint8), "arq0", *tx)
-    send(0, R("ls", 0)[:, 0:C], T.xs0[:, 0:C], "arq0", *tx)
-
-    t_tq, t_rp, tX, tkp, tkk = [], [()] * 4, [], None, None
     for r in range(ROUNDS):
-        last = r + 1 == ROUNDS
-        xq, xs, lst, sm, mg, vl, zl = R("xq", r), R("xs", r), T.lst, T.sm, T.mg, R("vl", r), R("zl", r)
-        lk, lv, lz = R("lk", r), R("lv", r), R("lz", r)
-        arq, ark, arv, arz = ("arq%d" % r, 16), ("ark%d" % r, 8), ("arv%d" % r, 8), ("arz%d" % r, 8)
+        for n, sem, k in (("lq", "arq", 16), ("ls", "arq", 16), ("lv", "arv", 8), ("la", "ara", 8)):
+            wrote["%s%d" % (n, r)].append((cols("%s%d" % (n, r)), ("%s%d" % (sem, r), k)))
 
-        def own(b): return mm(bank(T.psa, b), T.eq[:, w128(b)], T.es[:, w128(b)], xq[:, 0:C], xs[:, 0:C], te[b], *tx, *t_rp[b])
+    def pl(name, b, lo=0, hi=C): return cols(name, C * b + lo, C * b + hi)
+    def bank(ps, b, n=C): return cols(ps, 512 * b, 512 * b + n)
+    def w128(name, b): return cols(name, 128 * b, 128 * b + 128)
+    def half(name, h, k=1): return cols(name, k * H * h, k * H * (h + 1))
+    def ends(name, n=C): return cols(name, 15, n, 16)
+    def gather(o, win, lst): return lambda q: cp(q, cols(o), by(cols(win), cols(lst)))
+    def wrap(o, x): return lambda q: vscan(cols(o), cols("wts", 0, C), cols(x))
+    def first(o, z): return lambda q: vts2(cols(o), ends(z), cols("invk"), Op.mult, H + 0.05, Op.add)
+    def both(k, z): return lambda q: vts2(cols("full", k, 40, 2), ends(z), cols("inv"), Op.mult, float(H * TWO), Op.add)
+    def unpack(ps, xq, xs): return lambda q: [mm(bank(ps, b), w128("eq", b), w128("es", b), cols(xq), cols(xs)) for b in range(4)]
+    def four(name, make): return {name + str(b): (lambda q, b=b: make(q, b)) for b in range(4)}
 
-        ps = [mm(T.psb[:, 512 * h:512 * h + H], T.uq2[:], T.us2[:], xq[:, H * h:H * h + H], xs[:, H * h:H * h + H], tx[h], tu1, tu2, *t_tq) for h in (0, 1)]
-        if r:
-            pt = [own(b) for b in range(4)]
-        fill()
-        ts = [vcp(T.sc[:, 0:H], T.psb[:, 0:H], ps[0]), acp(T.sc[:, H:C], T.psb[:, 512:512 + H], ps[1])]
-        if r:
-            tkp = scanx(4 + r, None, tx_kp)
-        tl = st["l"]
-        tga = acp(T.ga[:], T.sc[:, 0:C].indirect(lst[:, 20:40]), *ts, tl)
-        tgb1 = acp(T.gb[:, H:C], T.sc[:, 0:C].indirect(lst[:, 10:20]), *ts, tl)
-        tgb0 = vcp(T.gb[:, 0:H], T.sc[:, 0:C].indirect(lst[:, 0:10]), *ts, tl)
-        ttp, kps = {}, {}
-        if r:
-            tkp = readx(4 + r, R("kp", r)[:], tkp)
-            send(r, R("lk", r)[:], R("kp", r)[:], "ark%d" % r, tkp)
-            tpir = acp(T.pir[:], gat(T.crep, R("kp", r)), tkp)
-            for b in range(3):
-                ttp[b] = acp(T.tp[:, pl(b)], bank(T.psa, b), pt[b], *tX)
-        else:
-            tpp = acp(T.pp[:], gat(T.am, T.pu), tam)
-            def q1(): kps[2] = scanx(1, None, tx_kp)
-            def q2(): kps[3] = readx(1, R("kp", 0)[:], kps[2])
-            later.extend([q1, lambda: unpacker(0), q2] + [lambda b=b: unpacker(b) for b in range(1, 4)])
-            fill(1)
-        tb0 = vtt(T.bits[:, 0:H], T.sc[:, 0:C].indirect(lst[:, 40:50]), T.gb[:, 0:H], Op.is_le, tgb0)
-        tb2 = vtt(T.bits[:, C:2 * C], T.sc[:, 0:C].indirect(lst[:, 60:80]), T.ga[:], Op.is_le, tga)
-        tb1 = vtt(T.bits[:, H:C], T.sc[:, 0:C].indirect(lst[:, 50:60]), T.gb[:, H:C], Op.is_le, tgb1)
-        fill(1)
-        tz = vscan(T.zz[:], T.wts[:], T.bits[:], *twt, tb0, tb1, tb2)
-        fill(1)
-        e1 = vts(sm[:, 180:220], T.zz[:, 15:2 * C:16], T.thr[:, 15:16], Op.is_ge, tz, tth)
-        fill(1)
-        e2 = vtt(sm[:, 220:240], sm[:, 180:200], sm[:, 200:220], Op.is_equal, e1)
-        fill(1)
-        e3 = vtt(sm[:, 240:260], sm[:, 220:240], sm[:, 160:180], Op.is_equal, e2, st["q"])
-        fill(1)
-        e4 = vtt(sm[:, 260:280], sm[:, 240:260], sm[:, 80:100], Op.mult, e3, st["d"])
-        f4 = vtt(sm[:, 300:320], sm[:, 240:260], sm[:, 100:120], Op.mult, e3, st["d"])
-        fill(1)
-        e5 = vtt(sm[:, 280:300], sm[:, 260:280], mg[:, 0:20], Op.add, e4)
-        f5 = vtt(sm[:, 320:340], sm[:, 300:320], mg[:, 20:40], Op.add, f4)
-        tvl = vcp(vl[:], sm[:, 280:300], e5)
-        tap = vcp(T.ap[:] if r else T.thu[:], sm[:, 320:340], f5)
-        if r == 0:
-            send(0, R("lk", 0)[:], R("kp", 0)[:], "ark0", kps[3])
-        send(r, R("lv", r)[:], vl[:], "arv%d" % r, tvl)
+    def scores(r, src):
+        xq, xs, sc = "xq%d" % r, "xs%d" % r, cols("sc")
+        a, b = cols("four", 0, 80, 2), cols("four", 1, 80, 2)
+        return {
+            "qa": lambda q: vqt(half(xq, 0), half(xs, 0), half(src, 0, 4)),
+            "qb": lambda q: vqt(half(xq, 1), half(xs, 1), half(src, 1, 4)),
+            "sendq": lambda q: (send(r, cols("lq%d" % r), cols(xq), "arq%d" % r, dt.uint8), send(r, cols("ls%d" % r), cols(xs), "arq%d" % r)),
+            "zp": wrap("zp", "pw"), "zm": wrap("zm", "mw"), "bo0": both(0, "zp"), "bo1": both(1, "zm"),
+            "sh": lambda q: vts(cols("four", 0, 40), cols("full"), TWO.bit_length() - 1, Op.logical_shift_right),
+            "an": lambda q: vts(cols("four", 40, 80), cols("full"), TWO - 1, Op.bitwise_and),
+            "mn": lambda q: vtt(cols("lh", 0, 40), a, b, Op.min),
+            "mx": lambda q: vtt(cols("lh", 40, 80), a, b, Op.max),
+            "lst": lambda q: vcp(cols("lst"), cols("lh")),
+            "dd": lambda q: vtt(cols("dd"), cols("four", 1, 40, 2), cols("four", 0, 40, 2), Op.subtract),
+            "al": lambda q: vts2(cols("ch", 101, 200, 5), cols("dd"), -1.0, Op.max, 1.0, Op.min),
+            "dif": lambda q: vtt(cols("ch", 102, 200, 5), cols("lh", 20, 40), cols("lh", 60, 80), Op.subtract),
+            "sum": lambda q: vtt(cols("ch", 4, 100, 5), cols("lh", 20, 40), cols("lh", 60, 80), Op.add),
+            "S0": lambda q: mm(bank("psb", 0, H), cols("uq2"), cols("us2"), half(xq, 0), half(xs, 0)),
+            "S1": lambda q: mm(bank("psb", 1, H), cols("uq2"), cols("us2"), half(xq, 1), half(xs, 1)),
+            "s0": lambda q: cp(q, half("sc", 0), bank("psb", 0, H)),
+            "s1": lambda q: cp(q, half("sc", 1), bank("psb", 1, H)),
+            "T": unpack("psa", xq, xs), **four("t", lambda q, b: cp(q, pl("tp", b), bank("psa", b))),
+            "lo1a": lambda q: cp(q, half("gb", 0), by(sc, cols("lst", 0, 10))),
+            "lo1b": lambda q: cp(q, half("gb", 1), by(sc, cols("lst", 10, 20))),
+            "lo2": lambda q: cp(q, cols("ga"), by(sc, cols("lst", 20, 40))),
+            "hi1a": lambda q: vtt(half("bits", 0), by(sc, cols("lst", 40, 50)), half("gb", 0), Op.is_le),
+            "hi1b": lambda q: vtt(half("bits", 1), by(sc, cols("lst", 50, 60)), half("gb", 1), Op.is_le),
+            "hi2": lambda q: vtt(cols("bits", C, 2 * C), by(sc, cols("lst", 60, 80)), cols("ga"), Op.is_le),
+            "bscan": lambda q: vscan(cols("zz"), cols("wts"), cols("bits")),
+            "sig": lambda q: vts2(cols("ch", 0, 200, 5), ends("zz", 2 * C), cols("inv"), Op.mult, 0.5, Op.subtract),
+            "chain": lambda q: vscan(cols("cho"), cols("ch", 99, 199), cols("ch", 0, 100)),
+            "l1": lambda q: vts2(cols("vl%d" % r), cols("cho", 4, 100, 5), 0.5, Op.mult, 0.05, Op.add),
+            "sendl": lambda q: send(r, cols("lv%d" % r), cols("vl%d" % r), "arv%d" % r)}
 
-        def neighbour(): return [mm(bank(T.psb, b), T.eq[:, w128(b)], T.es[:, w128(b)], R("lq", r)[:], R("ls", r)[:], arq, *ts) for b in range(4)]
-        tq, tk, tv = {}, {}, {}
-
-        def pick(b): tk[b] = acp(T.tk[:, pl(b)], T.tq[:, pl(b)].indirect(lk[:, 0:20]), tq[b], ark)
-        def aevac(b): tq[b] = asc(T.tq[:, pl(b)], bank(T.psb, b), 0.5, pq[b])
-        def vevac(b): tq[b] = vts(T.tq[:, pl(b)], bank(T.psb, b), 0.5, Op.mult, pq[b])
-        def addv(b): tv[b] = vtt(T.vp[:, pl(b)], T.tq[:, pl(b)].indirect(lv[:, 0:20]), T.tk[:, pl(b)], Op.add, tq[b], tk[b], arv)
-        def zcols(b, c0, c1): return T.zt[:, 4 * c0 + b:4 * c1:4], T.vp[:, pl(b)].indirect(lz[:, c0 // 16:c1 // 16])
-
-        table = T.idf if last else T.w0
-
-        def next_lists():
-            def m(): st["m"] = vtt(T.bg[:, 0:C], gat(T.f1, T.ciu), T.mask[:], Op.mult, tf1, tci["u"])
-            def n0(): st[0] = vscan(T.bg[:, C:2 * C], T.keep[:], T.bg[:, 0:C], st["m"])
-            def n1(): st[1] = vcp(T.mg[:, 40:60], T.bg[:, C + 15:2 * C:16], st[0])
-            def n2(): st[2] = vts(T.mg[:, 0:20], T.mg[:, 40:60], 9, Op.logical_shift_right, st[1])
-            def n3(): st[3] = vts(T.mg[:, 20:40], T.mg[:, 40:60], 511, Op.bitwise_and, st[1])
-            def n4(): st[4] = vcp(T.m2u[:], T.mg[:, 0:20], st[2])
-            return [m, n0, n1, n2] + ([n4] if r else []) + [n3] + rest(T.jc, lambda: (tj, tci["f"]), lambda: (st[2], st[3]))
-
-        if r == 0:
-            later.extend(inverse())
-            pt = [own(b) for b in range(4)]
-            for b in range(3):
-                ttp[b] = acp(T.tp[:, pl(b)], bank(T.psa, b), pt[b])
-            tt0 = acp(T.tpr[:], gat(T.pp, T.thu), tpp, tap)
-            tthb = acp(T.thb[:], gat(T.idb, T.thu), tap)
-            pq = neighbour()
-            tph = acp(T.ph[:, 0:C], gat(T.idb, vl), tvl, i_b)
-            tkk = acp(T.ph[:, C:2 * C], T.ph[:, 0:C].indirect(vl[:, 0:20]), tph)
-            aevac(0)
-            aevac(1)
-            pick(0)
-            fill()
-            pick(1)
-            s, a, b, c = wrap16(T.tpr[:, 0:C], T.ciu[:, 0:20], zl[:], 0, tt0, tci["u"])
-            s2, a2, b2, c2 = wrap16(T.thb[:, 0:C], T.ciu[:, 0:20], T.ap[:], 2 * C, tthb, tci["u"])
-            a()
-            tci["f"] = vcp(T.jc[:, 20:40], T.ciu[:], tci["u"])
-            b()
-            c()
-            tzl = s[3]
-            send(0, R("lz", 0)[:], zl[:], "arz0", tzl)
-            a2()
-            tw0 = vtt(T.w0[:], gat(T.id512, T.cu), T.idf[:], Op.add, i_5, i_f, tcu)
-            b2()
-            vevac(2)
-            c2()
-            vevac(3)
-            tap = s2[3]
-            pick(2)
-            pick(3)
-            tf0 = acp(T.f0[:], gat(table, vl), tvl, tw0)
-        else:
-            pq = neighbour()
-            fill()
-            s, a, b, c = wrap16(T.pir[:, 0:C], vl[:, 0:20], zl[:], 0, tpir, tvl)
-            a()
-            b()
-            c()
-            tzl = s[3]
-            send(r, R("lz", r)[:], zl[:], "arz%d" % r, tzl)
-            tf0 = acp(T.f0[:], gat(table, vl), tvl, tw0, i_f)
-            if last:
-                tvq = vqt(T.vq[:], T.vs[:], T.vin[:], dv)
-            else:
-                tph = acp(T.ph[:, 0:C], gat(T.idb, vl), tvl, i_b)
-            aevac(0)
-            vevac(1)
-            pick(0)
-            vevac(2)
-            pick(1)
-            vevac(3)
-            pick(2)
-            pick(3)
+    def layer(r):
+        vl, a1, lv, la = ["%s%d" % (n, r) for n in ("vl", "ap", "lv", "la")]
+        def z(b, lo, hi): return lambda q: cp(q, cols("zt", 4 * lo + b, 4 * hi, 4), by(pl("vp", b), cols(la, lo // 16, hi // 16)), 0.5)
+        def qz(lo, hi): return lambda q: vqt(cols("zq", lo, hi), cols("zs", lo, hi), cols("zt", 4 * lo, 4 * hi))
+        steps = {
+            "scat": lambda q: vcp(by(cols("ar"), cols(vl)), cols("pw")), "ascan": wrap("za", "ar"), "a1": first(a1, "za"),
+            "senda": lambda q: send(r, cols(la), cols(a1), "ara%d" % r),
+            "f0": gather("f0", "w0" if r + 1 < ROUNDS else "idf", vl), "kco": gather("kco", "f0", a1), "g1": gather("g1", "f0", "pwu"),
+            "f1": gather("f1", "f0", a1), "f2": gather("f2", "f1", a1), "ze": wrap("ze", "f2"), "eu": first("eu", "ze"),
+            "pw": gather("pw", "g1", "eu"), "mw": gather("mw", "f0", "eu"), "pwu": first("pwu", "zp"),
+            "Tn": unpack("psb", "lq%d" % r, "ls%d" % r), **four("o", lambda q, b: cp(q, pl("tq", b), bank("psb", b))),
+            **four("tw", lambda q, b: cp(q, pl("tk", b), pl("tq", b))), **four("pk", lambda q, b: cp(q, pl("tk", b), by(pl("tq", b), cols(lv)))),
+            **four("v", lambda q, b: vtt(pl("vp", b), by(pl("tq", b), cols(lv)), pl("tk", b), Op.add) if b < 2 else vtt(pl("vp", b), pl("tk", b), bank("psb", b), Op.add)),
+            "qh": qz(HZ, C), "ql": qz(0, HZ),
+            **four("R", lambda q, b: mm(bank("psb", b), w128("wq", b), w128("wsc", b), cols("zq"), cols("zs"))),
+            **four("r", lambda q, b: cp(q, pl("rp", b), bank("psb", b), 0.03125)),
+            **four("x", lambda q, b: vtt(cols("xt", b, 4 * C, 4), by(pl("rp", b), cols(a1)), pl("tp", b), Op.add))}
         for b in range(4):
-            addv(b)
-        t_tq = [tq[b] for b in range(4)]
-        za = [acp(*zcols(0, 0, C), tv[0], arz), acp(*zcols(1, 0, C), tv[1]), acp(*zcols(2, 0, HZ), tv[2])]
-        zv = [vcp(*zcols(2, HZ, C), tv[2], arz), vcp(*zcols(3, HZ, C), tv[3]), vcp(*zcols(3, 0, HZ), tv[3])]
-        tz1 = vqt(T.zq[:, HZ:C], T.zs[:, HZ:C], T.zt[:, 4 * HZ:4 * C], *zv, za[1])
-        tz0 = vqt(T.zq[:, 0:HZ], T.zs[:, 0:HZ], T.zt[:, 0:4 * HZ], *zv, *za)
-        if last:
-            tco = acp(T.kco[:], gat(T.f0, zl), tf0, tzl)
-            need("S", [tco])
-            g.sync.dma_start(T.co[:], T.kco[0:128:16, :]).then_inc(T.sem.ost, 16)
-        else:
-            tf1 = acp(T.f1[:], gat(T.f0, zl), tf0, tzl)
-            later.extend(next_lists())
-        order = [0, 1, 3, 2]
-        pr, tr = {}, {}
-        for b in order:
-            pr[b] = mm(bank(T.psb if b == 3 else T.psa, b), T.wq[:, w128(b)], T.wsc[:, w128(b)], T.zq[:], T.zs[:], dwc, dws, tz0, tz1, tq[3] if b == 3 else ttp[b])
-        fill(2)
-        for b in order:
-            tr[b] = asc(T.rp[:, pl(b)], bank(T.psb if b == 3 else T.psa, b), 0.03125, pr[b], *tX)
-        trg = acp(T.rg[:], T.rp[:, pl(3)].indirect(T.ap[:, 0:20]), tr[3], tap)
-        tX = []
-        for b in range(3):
-            tX.append(vtt(T.xt[:, b:4 * C:4], T.rp[:, pl(b)].indirect(T.ap[:, 0:20]), T.tp[:, pl(b)], Op.add, tr[b], ttp[b], tap))
-            fill(1)
-        tX.append(vtt(T.xt[:, 3:4 * C:4], T.rg[:], bank(T.psa, 3), Op.add, trg, pt[3]))
-        t_rp = [[tr[0]], [tr[1]], [tr[2]], [tX[3]]]
-        t_tq = t_tq + [tr[3]]
-        if not last:
-            if r == 0:
-                tkk = acp(T.ph[:, 2 * C:3 * C], T.ph[:, C:2 * C].indirect(zl[:, 0:20]), tkk, tzl)
-            else:
-                tkk = acp(T.ph[:, 2 * C:3 * C], T.ph[:, 0:C].indirect(T.m2u[:, 0:20]), tph, st[4])
-            tkk = acp(T.ph[:, 3 * C:4 * C], T.ph[:, 2 * C:3 * C].indirect((vl if r else T.ap)[:, 0:20]), tkk, tap)
-            tx_kp = pickx(5 + r, T.ph[:, 3 * C:4 * C], T.ciu[:, 0:20], tkk)
-        nq, ns = R("xq", r + 1), R("xs", r + 1)
-        tx = [vqt(nq[:, h:h + H], ns[:, h:h + H], T.xt[:, 4 * h:4 * (h + H)], *tX) for h in (0, H)]
-        if not last:
-            n = r + 1
-            send(n, R("lq", n)[:, 0:C].bitcast(dt.uint8), nq[:, 0:C].bitcast(dt.uint8), "arq%d" % n, *tx)
-            send(n, R("ls", n)[:, 0:C], ns[:, 0:C], "arq%d" % n, *tx)
+            for piece, ps, lo, hi in (("h", "psa", HZ, C), ("l", "psb", 0, HZ)):
+                steps["R%d%s" % (b, piece)] = lambda q, b=b, ps=ps, lo=lo, hi=hi: mm(bank(ps, b, hi - lo), w128("wq", b), w128("wsc", b), cols("zq", lo, hi), cols("zs", lo, hi))
+                steps["r%d%s" % (b, piece)] = lambda q, b=b, ps=ps, lo=lo, hi=hi: cp(q, pl("rp", b, lo, hi), bank(ps, b, hi - lo), 0.03125)
+            steps.update({"z%d" % b: z(b, 0, C), "z%dh" % b: z(b, HZ, C), "z%dl" % b: z(b, 0, HZ)})
+        return steps
 
-    need("S", tx)
-    g.sync.dma_start(T.oc[:, 0:4 * C], T.xq3[:, 0:C].bitcast(dt.uint8)).then_inc(T.sem.ost, 16)
-    for k in range(4):
-        g.sync.dma_start(T.osc[4 * k:4 * k + 4, 0:C], T.xs3[32 * k:32 * k + 4, 0:C]).then_inc(T.sem.ost, 16)
-    py = [mm(T.psb[:, 512 * h:512 * h + H], T.vq[:], T.vs[:], T.xq3[:, H * h:H * h + H], T.xs3[:, H * h:H * h + H], tx[h], tvq, *t_tq) for h in (0, 1)]
-    ty0 = vcp(T.yt[:, 0:H], T.psb[:, 0:H], py[0])
-    ty1 = acp(T.yt[:, H:C], T.psb[:, 512:512 + H], py[1])
-    need("S", [ty0])
-    g.sync.dma_start(T.y[:, 0:H], T.yt[:, 0:H]).then_inc(T.sem.ost, 16)
-    need("A", [ty1])
-    g.scalar.dma_start(T.y[:, H:C], T.yt[:, H:C]).then_inc(T.sem.ost, 16)
+    def play(order, steps):
+        for name in order.split():
+            steps[name.split(".")[0]]("V" if name.endswith(".V") else "A")
+
+    load("A", "pl", cols("pi32"), T.pl[:])
+    load("S", "ml", cols("mi32"), T.ml[:])
+    load("A", "cl", cols("ci32"), T.cl[:])
+    load("S", "x0", half("xin", 0, 4), T.x[:, 0:4 * H])
+    load("A", "x1", half("xin", 1, 4), T.x[:, 4 * H:4 * C])
+    load("S", "u", cols("uin"), T.u[:])
+    load("S", "wc", cols("wq"), T.wc[:], dt.uint8)
+    load("S", "ws", cols("wsc"), T.ws[:])
+    load("S", "v", cols("vin"), T.v[:])
+
+    iota("pcol", [1, [0, 1]])
+    iota("t16", [0, [1, 16]])
+    iota("idk", [0, [TWO, C]], -H * TWO)
+    iota("idf", [0, [1, C]])
+    vfill(cols("ein"), 1.0)
+    vfill(cols("ch"), 0.0)
+    run("G", [cols("ein")], [cols("ein")], lambda: g.affine_select(T.ein[:], T.ein[:], [[1, 516]], Op.is_equal, 0.0, -3, -4))
+    iota("pk", [0, [16, 8]])
+    vts(cols("qi"), cols("pcol"), 15, Op.bitwise_and)
+    vfill(cols("ch", 103, 200, 5), 4.0)
+    vts(cols("q1"), cols("qi"), 1.0, Op.add)
+    vts2(cols("inv"), cols("qi"), 15.0, Op.is_equal, 1.0 / BIG, Op.max)
+    vts(cols("invk"), cols("inv"), 1.0 / TWO, Op.mult)
+    vfill(cols("z40"), 0.0)
+    vcp(cols("qf"), cols("qi"))
+    vts(cols("wa"), cols("t16"), cols("q1"), Op.is_gt)
+    vts2(cols("wb"), cols("t16"), cols("q1"), Op.is_equal, BIG, Op.mult)
+    vts(cols("qu"), cols("z40"), cols("qf"), Op.add)
+    vtt(cols("w16"), cols("wa"), cols("wb"), Op.add)
+    cp("A", cols("wts"), by(cols("w16"), cols("qu")))
+
+    play(START, {
+        **scores(0, "xin"),
+        "cu": lambda q: vcp(cols("cu"), cols("ci32")), "pu": lambda q: vcp(cols("pu"), cols("pi32")), "mu": lambda q: vcp(cols("mu"), cols("mi32")),
+        "ai": lambda q: vcp(by(cols("ar"), cols("pu")), cols("idk")),
+        "g1": gather("g1", "ar", "mu"), "g2": gather("f2", "g1", "pu"), "ze": wrap("ze", "f2"), "pwu": first("pwu", "ze"),
+        "w0": lambda q: vtt(cols("w0"), by(cols("idf"), cols("cu")), cols("idk"), Op.add),
+        "f1": gather("f1", "w0", "mu"), "pw": gather("pw", "w0", "pwu"), "mw": gather("mw", "f1", "pwu"),
+        **four("e", lambda q, b: vqt(w128("eq", b), w128("es", b), cols("ein", 3 - b, 515 - b))),
+        "uq": lambda q: vqt(cols("uq"), cols("us"), cols("uin")), "pku": lambda q: vcp(cols("pku"), cols("pk")),
+        "us2": gather("us2", "us", "pku"), "uq2": lambda q: vcp(cols("uq2"), by(cols("uq"), cols("pku")), dt.uint32)})
+    for r in range(ROUNDS - 1):
+        play(MID, {**layer(r), **scores(r + 1, "xt")})
+    play(LAST, {
+        **layer(ROUNDS - 1), **scores(ROUNDS, "xt"),
+        "vq": lambda q: vqt(cols("vq"), cols("vs"), cols("vin")),
+        "co": lambda q: store("S", T.co[:], cols("kco"), T.kco[0:128:16, :]),
+        "oc": lambda q: store("S", T.oc[:, 0:4 * C], cols("xq3"), T.xq3[:, 0:C].bitcast(dt.uint8)),
+        "osc": lambda q: [store("S", T.osc[4 * k:4 * k + 4, 0:C], cols("xs3"), T.xs3[32 * k:32 * k + 4, 0:C]) for k in range(4)],
+        "Y0": lambda q: mm(bank("psb", 0, H), cols("vq"), cols("vs"), half("xq3", 0), half("xs3", 0)),
+        "Y1": lambda q: mm(bank("psb", 1, H), cols("vq"), cols("vs"), half("xq3", 1), half("xs3", 1)),
+        "y0": lambda q: cp(q, half("yt", 0), bank("psb", 0, H)), "y1": lambda q: cp(q, half("yt", 1), bank("psb", 1, H)),
+        "sy0": lambda q: store("S", T.y[:, 0:H], half("yt", 0), T.yt[:, 0:H]),
+        "sy1": lambda q: store("A", T.y[:, H:C], half("yt", 1), T.yt[:, H:C])})
     need("G", [(q, count[q]) for q in ("V", "A", "P", "G")])
-    g.wait_ge(T.sem.ost, 16 * 8)
+    g.wait_ge(T.sem.ost, stores[0])
     g.wait_ge(T.sem.sent, sent[0])

from concourse.mybir import dt, AluOpType as Op, ActivationFunctionType as Fn

C = 320
H = C // 2
STEP = [1, 2, 4]
ROUNDS = 3
HZ = 192
BIG = 2.0 ** 40
TWO = 2048
X4, F32, B16, I32, U16, U8 = "float8_e4m3fn_x4", "float32", "bfloat16", "int32", "uint16", "uint8"

SCRATCH = {}
for _names, _w, _d in (
        ("idf idk", C, F32), ("t16 wa wb w16", 16, B16), ("wts", 2 * C, B16), ("pcol qi", 1, I32), ("qf q1 inv invk", 1, F32), ("z40", 40, F32), ("qu", 40, U16),
        ("pk", 8, I32), ("pku", 8, U16), ("ein", 516, B16), ("eq", 512, X4), ("es", 512, U8),
        ("xin", 4 * C, B16), ("uin vin", 512, B16), ("ci32 mi32 pi32", 20, I32), ("cu mu pu", 20, U16),
        ("wq", 512, X4), ("wsc", 512, U8), ("uq uq2 vq", 128, X4), ("us us2 vs", 128, U8),
        ("w0 g1 pw mw f0 f1 zp zm", C, F32), ("ar za f2 ze", C, B16), ("pwu eu", 20, U16), ("full", 40, I32), ("four", 80, I32), ("lh", 80, F32), ("dd", 20, F32),
        ("lst", 80, U16), ("ch", 200, F32), ("cho", 100, F32),
        ("sc ga gb kco yt rg", C, F32), ("bits zz", 2 * C, B16),
        ("tp vp rp", 4 * C, F32), ("tq tk zt xt", 4 * C, B16), ("zq", C, X4), ("zs", C, U8)):
    for _n in _names.split():
        SCRATCH[_n] = ("sbuf", [128, _w], _d)
for _r in range(ROUNDS + 1):
    SCRATCH["xq%d" % _r] = ("sbuf", [128, C], X4)
    SCRATCH["xs%d" % _r] = ("sbuf", [128, C], U8)
for _r in range(ROUNDS):
    SCRATCH["lq%d" % _r] = ("sbuf", [128, C], X4)
    SCRATCH["ls%d" % _r] = ("sbuf", [128, C], U8)
    for _n in ("lv", "la", "vl", "ap"):
        SCRATCH["%s%d" % (_n, _r)] = ("sbuf", [128, 20], U16)
SCRATCH["psa"] = ("psum", [128, 2048], F32)
SCRATCH["psb"] = ("psum", [128, 2048], F32)

LOADS = ["x0", "x1", "u", "v", "cl", "pl", "ml", "wc", "ws"]
SEMAPHORES = ["V", "A", "P", "G", "sent", "ost"] + ["d" + k for k in LOADS] + ["%s%d" % (k, r) for k in ("arq", "arv", "ara") for r in range(ROUNDS)]

START = """pu ai mu g1 g2 qa cu qb sendq w0 pku ze e3 pwu e2 uq e1 f1 e0 uq2 pw zp mw zm us2 S0 S1 T bo0 bo1 an sh mn mx s0 dd lst s1
           lo2 sum lo1b.V al hi1b hi2 lo1a hi1a t3 t2 dif bscan sig chain l1 sendl t0 t1"""
MID = """f0 scat ascan g1 a1 senda f1 Tn f2 o0.V o2 o1.V tw0.V tw1.V ze v0 eu o3 pk2 v1 pk3 v2 v3
         z2l.V z3l.V mw z0 z1 z2h.V z3h ql qh R0 R1 R2 R3 zm pw zp bo1 bo0 an r0 x0 r1 x1 r2 x2 r3 x3 sh qa S0 qb sendq S1 T
         mn mx dd lst s1.V al s0 lo2 lo1a.V lo1b sum hi1a t0 t1 hi2 hi1b bscan dif t2 sig chain pwu l1 sendl t3"""
LAST = """scat ascan a1 senda f0 Tn o0 o2 o3 pk2 o1.V tw0.V vq pk3 tw1.V v0 v1 z0 z1 v2 v3 z3h z2l.V z3l.V z2h.V kco co ql qh
          R0 R1 R2 R3 r0.V x0 r1 x1 r2 x2 r3 x3 qb Y1 qa Y0 oc y1.V sy1 y0.V sy0 osc"""


def cols(name, lo=0, hi=None, step=1):
    return (name, lo, SCRATCH[name][1][1] if hi is None else hi, step)


def by(win, lst):
    return (win, lst)


def rank_program(g, core, T, topo):
    rank = T.rank_of(core)
    if rank is None:
        return
    queues = {"V": g.vector, "A": g.scalar, "P": g.tensor, "G": g, "S": g.sync}
    count = {k: 0 for k in queues}
    seen = {k: {} for k in queues}
    known = {}
    wrote = {n: [] for n in SCRATCH}
    read = {n: [] for n in SCRATCH}

    def need(q, marks):
        for sem, val in sorted(set(marks), key=lambda t: -t[1]):
            if seen[q].get(sem, 0) >= val:
                continue
            queues[q].wait_ge(T.sem[sem], val)
            seen[q][sem] = val
            for s2, v2 in known.get((sem, val), {}).items():
                if seen[q].get(s2, 0) < v2:
                    seen[q][s2] = v2

    def meet(a, b):
        if a[2] <= b[1] or b[2] <= a[1]:
            return False
        return a[3] != b[3] or (a[1] - b[1]) % a[3] == 0

    def touch(outs, ins):
        w, r = [], []
        for o in outs:
            w.append(o if len(o) == 4 else o[0])
            r += [] if len(o) == 4 else [o[1]]
        for i in ins:
            r += [i] if len(i) == 4 else list(i)
        bank = lambda v: (v[0], v[1] // 512 * 512, v[1] // 512 * 512 + 512, 1)
        w = [bank(v) if v[0][:2] == "ps" else v for v in w] + [bank(v) for v in r if v[0][:2] == "ps"]
        return w, [v for v in r if v[0][:2] != "ps"]

    def before(w, r):
        return [m for v in w + r for u, m in wrote[v[0]] if meet(u, v)] + [m for v in w for u, m in read[v[0]] if meet(u, v)]

    def ap(v, cast=None):
        if not isinstance(v, tuple):
            return v
        if len(v) == 2:
            return ap(v[0], cast).indirect(ap(v[1]))
        a = T[v[0]][:, v[1]:v[2]:v[3]] if v[3] > 1 else T[v[0]][:, v[1]:v[2]]
        return a.bitcast(cast) if cast else a

    def run(q, outs, ins, call):
        w, r = touch(outs, [i for i in ins if isinstance(i, tuple)])
        need(q, before(w, r))
        call().then_inc(T.sem[q], 1)
        count[q] += 1
        known[(q, count[q])] = dict(seen[q])
        for v in w:
            wrote[v[0]].append((v, (q, count[q])))
        for v in r:
            read[v[0]].append((v, (q, count[q])))

    def vfill(o, k): run("V", [o], [], lambda: g.vector.memset(ap(o), k))
    def vcp(o, i, cast=None): run("V", [o], [i], lambda: g.vector.tensor_copy(ap(o, cast), ap(i, cast)))
    def vtt(o, a, b, op): run("V", [o], [a, b], lambda: g.vector.tensor_tensor(ap(o), ap(a), ap(b), op))
    def vts(o, a, s, op): run("V", [o], [a, s], lambda: g.vector.tensor_scalar(ap(o), ap(a), ap(s), None, op))
    def vts2(o, a, s, op, s2, op2): run("V", [o], [a, s, s2], lambda: g.vector.tensor_scalar(ap(o), ap(a), ap(s), ap(s2), op, op2))
    def vscan(o, w, x): run("V", [o], [w, x], lambda: g.vector.tensor_tensor_scan(ap(o), ap(w), ap(x), 0.0, Op.mult, Op.add))
    def vqt(o, s, x): run("V", [o, s], [x], lambda: g.vector.quantize_mx(ap(o), ap(s), ap(x)))
    def mm(o, w, ws, x, xs): run("P", [o], [w, ws, x, xs], lambda: g.tensor.matmul_mx(ap(o), ap(w), ap(ws), ap(x), ap(xs), True, True))

    def cp(q, o, i, k=None):
        if q == "V":
            vcp(o, i) if k is None else vts(o, i, k, Op.mult)
        else:
            run("A", [o], [i], lambda: g.scalar.activation(ap(o), ap(i), Fn.Copy, **({} if k is None else {"scale": k})))

    def iota(o, pattern, base=0):
        kw = {} if SCRATCH[o][2] == I32 else {"allow_small_or_imprecise_dtypes": True}
        run("G", [cols(o)], [], lambda: g.iota(T[o][:], pattern[1:], base, pattern[0], **kw))

    def load(q, name, o, src, cast=None):
        queues[q].dma_start(ap(o, cast), src).then_inc(T.sem["d" + name], 16)
        wrote[o[0]].append((o, ("d" + name, 16)))

    stores = [0]

    def store(q, out, v, src):
        need(q, before([], [v]))
        queues[q].dma_start(out, src).then_inc(T.sem.ost, 16)
        stores[0] += 16

    sent = [0]

    def send(r, land, src, sem, cast=None):
        need("G", before([], [src]))
        dst = T.cores[(rank + STEP[r]) % len(T.cores)]
        rid, pid, _ = topo.addr(dst)
        eng = topo.engines(core, dst)[:8]
        g.remote_dma(ap(land, cast), ap(src, cast), T.sem[sem], T.sem.sent, pid, rid, sum(1 << e for e in eng))
        sent[0] += len(eng)

    for r in range(ROUNDS):
        for n, sem, k in (("lq", "arq", 16), ("ls", "arq", 16), ("lv", "arv", 8), ("la", "ara", 8)):
            wrote["%s%d" % (n, r)].append((cols("%s%d" % (n, r)), ("%s%d" % (sem, r), k)))

    def pl(name, b, lo=0, hi=C): return cols(name, C * b + lo, C * b + hi)
    def bank(ps, b, n=C): return cols(ps, 512 * b, 512 * b + n)
    def w128(name, b): return cols(name, 128 * b, 128 * b + 128)
    def half(name, h, k=1): return cols(name, k * H * h, k * H * (h + 1))
    def ends(name, n=C): return cols(name, 15, n, 16)
    def gather(o, win, lst): return lambda q: cp(q, cols(o), by(cols(win), cols(lst)))
    def wrap(o, x): return lambda q: vscan(cols(o), cols("wts", 0, C), cols(x))
    def first(o, z): return lambda q: vts2(cols(o), ends(z), cols("invk"), Op.mult, H + 0.05, Op.add)
    def both(k, z): return lambda q: vts2(cols("full", k, 40, 2), ends(z), cols("inv"), Op.mult, float(H * TWO), Op.add)
    def unpack(ps, xq, xs): return lambda q: [mm(bank(ps, b), w128("eq", b), w128("es", b), cols(xq), cols(xs)) for b in range(4)]
    def four(name, make): return {name + str(b): (lambda q, b=b: make(q, b)) for b in range(4)}

    def scores(r, src):
        xq, xs, sc = "xq%d" % r, "xs%d" % r, cols("sc")
        a, b = cols("four", 0, 80, 2), cols("four", 1, 80, 2)
        return {
            "qa": lambda q: vqt(half(xq, 0), half(xs, 0), half(src, 0, 4)),
            "qb": lambda q: vqt(half(xq, 1), half(xs, 1), half(src, 1, 4)),
            "sendq": lambda q: (send(r, cols("lq%d" % r), cols(xq), "arq%d" % r, dt.uint8), send(r, cols("ls%d" % r), cols(xs), "arq%d" % r)),
            "zp": wrap("zp", "pw"), "zm": wrap("zm", "mw"), "bo0": both(0, "zp"), "bo1": both(1, "zm"),
            "sh": lambda q: vts(cols("four", 0, 40), cols("full"), TWO.bit_length() - 1, Op.logical_shift_right),
            "an": lambda q: vts(cols("four", 40, 80), cols("full"), TWO - 1, Op.bitwise_and),
            "mn": lambda q: vtt(cols("lh", 0, 40), a, b, Op.min),
            "mx": lambda q: vtt(cols("lh", 40, 80), a, b, Op.max),
            "lst": lambda q: vcp(cols("lst"), cols("lh")),
            "dd": lambda q: vtt(cols("dd"), cols("four", 1, 40, 2), cols("four", 0, 40, 2), Op.subtract),
            "al": lambda q: vts2(cols("ch", 101, 200, 5), cols("dd"), -1.0, Op.max, 1.0, Op.min),
            "dif": lambda q: vtt(cols("ch", 102, 200, 5), cols("lh", 20, 40), cols("lh", 60, 80), Op.subtract),
            "sum": lambda q: vtt(cols("ch", 4, 100, 5), cols("lh", 20, 40), cols("lh", 60, 80), Op.add),
            "S0": lambda q: mm(bank("psb", 0, H), cols("uq2"), cols("us2"), half(xq, 0), half(xs, 0)),
            "S1": lambda q: mm(bank("psb", 1, H), cols("uq2"), cols("us2"), half(xq, 1), half(xs, 1)),
            "s0": lambda q: cp(q, half("sc", 0), bank("psb", 0, H)),
            "s1": lambda q: cp(q, half("sc", 1), bank("psb", 1, H)),
            "T": unpack("psa", xq, xs), **four("t", lambda q, b: cp(q, pl("tp", b), bank("psa", b))),
            "lo1a": lambda q: cp(q, half("gb", 0), by(sc, cols("lst", 0, 10))),
            "lo1b": lambda q: cp(q, half("gb", 1), by(sc, cols("lst", 10, 20))),
            "lo2": lambda q: cp(q, cols("ga"), by(sc, cols("lst", 20, 40))),
            "hi1a": lambda q: vtt(half("bits", 0), by(sc, cols("lst", 40, 50)), half("gb", 0), Op.is_le),
            "hi1b": lambda q: vtt(half("bits", 1), by(sc, cols("lst", 50, 60)), half("gb", 1), Op.is_le),
            "hi2": lambda q: vtt(cols("bits", C, 2 * C), by(sc, cols("lst", 60, 80)), cols("ga"), Op.is_le),
            "bscan": lambda q: vscan(cols("zz"), cols("wts"), cols("bits")),
            "sig": lambda q: vts2(cols("ch", 0, 200, 5), ends("zz", 2 * C), cols("inv"), Op.mult, 0.5, Op.subtract),
            "chain": lambda q: vscan(cols("cho"), cols("ch", 99, 199), cols("ch", 0, 100)),
            "l1": lambda q: vts2(cols("vl%d" % r), cols("cho", 4, 100, 5), 0.5, Op.mult, 0.05, Op.add),
            "sendl": lambda q: send(r, cols("lv%d" % r), cols("vl%d" % r), "arv%d" % r)}

    def layer(r):
        vl, a1, lv, la = ["%s%d" % (n, r) for n in ("vl", "ap", "lv", "la")]
        def z(b, lo, hi): return lambda q: cp(q, cols("zt", 4 * lo + b, 4 * hi, 4), by(pl("vp", b), cols(la, lo // 16, hi // 16)), 0.5)
        def qz(lo, hi): return lambda q: vqt(cols("zq", lo, hi), cols("zs", lo, hi), cols("zt", 4 * lo, 4 * hi))
        steps = {
            "scat": lambda q: vcp(by(cols("ar"), cols(vl)), cols("pw")), "ascan": wrap("za", "ar"), "a1": first(a1, "za"),
            "senda": lambda q: send(r, cols(la), cols(a1), "ara%d" % r),
            "f0": gather("f0", "w0" if r + 1 < ROUNDS else "idf", vl), "kco": gather("kco", "f0", a1), "g1": gather("g1", "f0", "pwu"),
            "f1": gather("f1", "f0", a1), "f2": gather("f2", "f1", a1), "ze": wrap("ze", "f2"), "eu": first("eu", "ze"),
            "pw": gather("pw", "g1", "eu"), "mw": gather("mw", "f0", "eu"), "pwu": first("pwu", "zp"),
            "Tn": unpack("psb", "lq%d" % r, "ls%d" % r), **four("o", lambda q, b: cp(q, pl("tq", b), bank("psb", b))),
            **four("tw", lambda q, b: cp(q, pl("tk", b), pl("tq", b))), **four("pk", lambda q, b: cp(q, pl("tk", b), by(pl("tq", b), cols(lv)))),
            **four("v", lambda q, b: vtt(pl("vp", b), by(pl("tq", b), cols(lv)), pl("tk", b), Op.add) if b < 2 else vtt(pl("vp", b), pl("tk", b), bank("psb", b), Op.add)),
            "qh": qz(HZ, C), "ql": qz(0, HZ),
            **four("R", lambda q, b: mm(bank("psb", b), w128("wq", b), w128("wsc", b), cols("zq"), cols("zs"))),
            **four("r", lambda q, b: cp(q, pl("rp", b), bank("psb", b), 0.03125)),
            **four("x", lambda q, b: vtt(cols("xt", b, 4 * C, 4), by(pl("rp", b), cols(a1)), pl("tp", b), Op.add))}
        for b in range(4):
            for piece, ps, lo, hi in (("h", "psa", HZ, C), ("l", "psb", 0, HZ)):
                steps["R%d%s" % (b, piece)] = lambda q, b=b, ps=ps, lo=lo, hi=hi: mm(bank(ps, b, hi - lo), w128("wq", b), w128("wsc", b), cols("zq", lo, hi), cols("zs", lo, hi))
                steps["r%d%s" % (b, piece)] = lambda q, b=b, ps=ps, lo=lo, hi=hi: cp(q, pl("rp", b, lo, hi), bank(ps, b, hi - lo), 0.03125)
            steps.update({"z%d" % b: z(b, 0, C), "z%dh" % b: z(b, HZ, C), "z%dl" % b: z(b, 0, HZ)})
        return steps

    def play(order, steps):
        for name in order.split():
            steps[name.split(".")[0]]("V" if name.endswith(".V") else "A")

    load("A", "pl", cols("pi32"), T.pl[:])
    load("S", "ml", cols("mi32"), T.ml[:])
    load("A", "cl", cols("ci32"), T.cl[:])
    load("S", "x0", half("xin", 0, 4), T.x[:, 0:4 * H])
    load("A", "x1", half("xin", 1, 4), T.x[:, 4 * H:4 * C])
    load("S", "u", cols("uin"), T.u[:])
    load("S", "wc", cols("wq"), T.wc[:], dt.uint8)
    load("S", "ws", cols("wsc"), T.ws[:])
    load("S", "v", cols("vin"), T.v[:])

    iota("pcol", [1, [0, 1]])
    iota("t16", [0, [1, 16]])
    iota("idk", [0, [TWO, C]], -H * TWO)
    iota("idf", [0, [1, C]])
    vfill(cols("ein"), 1.0)
    vfill(cols("ch"), 0.0)
    run("G", [cols("ein")], [cols("ein")], lambda: g.affine_select(T.ein[:], T.ein[:], [[1, 516]], Op.is_equal, 0.0, -3, -4))
    iota("pk", [0, [16, 8]])
    vts(cols("qi"), cols("pcol"), 15, Op.bitwise_and)
    vfill(cols("ch", 103, 200, 5), 4.0)
    vts(cols("q1"), cols("qi"), 1.0, Op.add)
    vts2(cols("inv"), cols("qi"), 15.0, Op.is_equal, 1.0 / BIG, Op.max)
    vts(cols("invk"), cols("inv"), 1.0 / TWO, Op.mult)
    vfill(cols("z40"), 0.0)
    vcp(cols("qf"), cols("qi"))
    vts(cols("wa"), cols("t16"), cols("q1"), Op.is_gt)
    vts2(cols("wb"), cols("t16"), cols("q1"), Op.is_equal, BIG, Op.mult)
    vts(cols("qu"), cols("z40"), cols("qf"), Op.add)
    vtt(cols("w16"), cols("wa"), cols("wb"), Op.add)
    cp("A", cols("wts"), by(cols("w16"), cols("qu")))

    play(START, {
        **scores(0, "xin"),
        "cu": lambda q: vcp(cols("cu"), cols("ci32")), "pu": lambda q: vcp(cols("pu"), cols("pi32")), "mu": lambda q: vcp(cols("mu"), cols("mi32")),
        "ai": lambda q: vcp(by(cols("ar"), cols("pu")), cols("idk")),
        "g1": gather("g1", "ar", "mu"), "g2": gather("f2", "g1", "pu"), "ze": wrap("ze", "f2"), "pwu": first("pwu", "ze"),
        "w0": lambda q: vtt(cols("w0"), by(cols("idf"), cols("cu")), cols("idk"), Op.add),
        "f1": gather("f1", "w0", "mu"), "pw": gather("pw", "w0", "pwu"), "mw": gather("mw", "f1", "pwu"),
        **four("e", lambda q, b: vqt(w128("eq", b), w128("es", b), cols("ein", 3 - b, 515 - b))),
        "uq": lambda q: vqt(cols("uq"), cols("us"), cols("uin")), "pku": lambda q: vcp(cols("pku"), cols("pk")),
        "us2": gather("us2", "us", "pku"), "uq2": lambda q: vcp(cols("uq2"), by(cols("uq"), cols("pku")), dt.uint32)})
    for r in range(ROUNDS - 1):
        play(MID, {**layer(r), **scores(r + 1, "xt")})
    play(LAST, {
        **layer(ROUNDS - 1), **scores(ROUNDS, "xt"),
        "vq": lambda q: vqt(cols("vq"), cols("vs"), cols("vin")),
        "co": lambda q: store("S", T.co[:], cols("kco"), T.kco[0:128:16, :]),
        "oc": lambda q: store("S", T.oc[:, 0:4 * C], cols("xq3"), T.xq3[:, 0:C].bitcast(dt.uint8)),
        "osc": lambda q: [store("S", T.osc[4 * k:4 * k + 4, 0:C], cols("xs3"), T.xs3[32 * k:32 * k + 4, 0:C]) for k in range(4)],
        "Y0": lambda q: mm(bank("psb", 0, H), cols("vq"), cols("vs"), half("xq3", 0), half("xs3", 0)),
        "Y1": lambda q: mm(bank("psb", 1, H), cols("vq"), cols("vs"), half("xq3", 1), half("xs3", 1)),
        "y0": lambda q: cp(q, half("yt", 0), bank("psb", 0, H)), "y1": lambda q: cp(q, half("yt", 1), bank("psb", 1, H)),
        "sy0": lambda q: store("S", T.y[:, 0:H], half("yt", 0), T.yt[:, 0:H]),
        "sy1": lambda q: store("A", T.y[:, H:C], half("yt", 1), T.yt[:, H:C])})
    need("G", [(q, count[q]) for q in ("V", "A", "P", "G")])
    g.wait_ge(T.sem.ost, stores[0])
    g.wait_ge(T.sem.sent, sent[0])
